import numpy as np
import ml_dtypes


def mxq(x, axis, fmt="e4m3"):
    dtype, down = {"e4m3": (ml_dtypes.float8_e4m3fn, 7), "e5m2": (ml_dtypes.float8_e5m2, 14)}[fmt]
    v = np.moveaxis(np.asarray(x, np.float32).astype(ml_dtypes.bfloat16).astype(np.float64), axis, -1)
    blocks = v.reshape(v.shape[:-1] + (-1, 32))
    amax = np.abs(blocks).max(-1, keepdims=True)
    byte = np.maximum(np.where(amax > 0, np.frexp(amax)[1] - 1 + 127, 0) - down, 1)
    scale = np.exp2(byte - 127.0)
    codes = (blocks / scale).astype(np.float32).astype(dtype).astype(np.float64)
    return np.moveaxis((codes * scale).reshape(v.shape), -1, axis)


WIDE = False


def mx_kscale(k):
    if not WIDE:
        return np.ones(k)
    levels = np.array([10, -10, 5, -5, 0])
    if k % 512:
        return np.exp2(np.random.permutation(np.resize(levels, k // 32))).repeat(32)
    a = np.empty((k // 512, 16))
    for p in range(k // 512):
        a[p, :8] = np.random.permutation(np.resize(levels, 8))
        for g in range(8):
            far = levels[np.abs(levels - a[p, g]) >= 10]
            a[p, g + 8] = far[np.random.randint(len(far))]
    return np.exp2(a.ravel()).repeat(32)


def f64(x):
    return np.asarray(x).astype(np.float64)


def striped(idx):
    return np.tile(np.asarray(idx).reshape(-1, 16).T, (8, 1)).astype(np.uint16)


def unstriped(offs):
    return offs[:16].T.reshape(-1).astype(np.int64)


E2M1 = np.array([0.0, 0.5, 1.0, 1.5, 2.0, 3.0, 4.0, 6.0, -0.0, -0.5, -1.0, -1.5, -2.0, -3.0, -4.0, -6.0])


def pack_weight(w, fmt):
    k, n = w.shape
    w = f64(np.asarray(w, np.float32).astype(ml_dtypes.bfloat16)).reshape(k // 32, 32, n)
    amax = np.abs(w).max(1)
    if fmt == "e4m3":
        byte = np.frexp(amax)[1] - 1 + 127 - 7
    else:
        mant, ex = np.frexp(amax / 6.0)
        byte = np.where(mant > 0.5, ex, ex - 1) + 127
    byte = np.clip(np.where(amax > 0, byte, 1), 1, 254)
    scaled = (w * np.exp2(127.0 - byte)[:, None, :]).reshape(k, n).astype(np.float32)
    by_word = np.ascontiguousarray(scaled.reshape(k // 512, 128, 4, n).transpose(0, 1, 3, 2))
    if fmt == "e4m3":
        words = by_word.astype(ml_dtypes.float8_e4m3fn).view(np.uint8)
    else:
        c = by_word.astype(ml_dtypes.float4_e2m1fn).view(np.uint8) & 0xF
        words = (c[..., 0::2] | (c[..., 1::2] << 4)).reshape(k // 512, 128, 2 * n)
    return np.ascontiguousarray(words), np.ascontiguousarray(byte.astype(np.uint8).reshape(k // 512, 16, n))


def unpack_weight(words, scales, fmt):
    g, _, n = scales.shape
    words = np.ascontiguousarray(words).reshape(g, 128, n, -1)
    if fmt == "e4m3":
        vals = words.view(ml_dtypes.float8_e4m3fn).astype(np.float64)
    else:
        nib = np.empty((g, 128, n, 4), np.uint8)
        nib[..., 0::2] = words & 0xF
        nib[..., 1::2] = words >> 4
        vals = E2M1[nib]
    vals = vals * np.repeat(np.exp2(scales.astype(np.float64) - 127.0), 8, axis=1)[..., None]
    return vals.transpose(0, 1, 3, 2).reshape(g * 512, n)


K, U, I, T, E = 512, 2048, 512, 1024, 512


def setup_inputs():
    n = np.random.standard_normal
    idx = np.random.permutation(U)[:I]
    idx2 = np.random.permutation(T)[:I]
    fk = mx_kscale(K)
    embp = pack_weight(n((K, U)) / fk[:, None], "e2m1")
    return {
        "emb_words": embp[0],
        "emb_scales": embp[1],
        "wv": (n((K, E)) * 1 / np.sqrt(K) * fk[:, None]).astype(np.float32),
        "old": (n((E, T))).astype(np.float32),
        "retain": (np.random.uniform(0.0, 1.0, (1, T))).astype(np.float32),
        "offs": striped(idx),
        "offs2": striped(idx2),
    }


def reference(emb_words, emb_scales, wv, old, retain, offs, offs2):
    idx = unstriped(offs)
    idx2 = unstriped(offs2)
    embu = unpack_weight(emb_words, emb_scales, "e2m1")
    wvq = mxq(f64(wv), 0, "e4m3")
    embidxg = embu[:, idx]
    v = wvq.T @ embidxg
    vf = np.zeros((E, T))
    vf[:, idx2] = v
    y = f64(old) * f64(retain) + vf
    return y

@@ -1,0 +1,195 @@
+from contextlib import ExitStack
+
+import concourse.mybir as mybir
+from concourse.masks import make_identity
+
+K, U, I, T, E = 512, 2048, 512, 1024, 512
+FLOPS = 2 * K * E * I
+
+F32 = mybir.dt.float32
+BF16 = mybir.dt.bfloat16
+I32 = mybir.dt.int32
+U32 = mybir.dt.uint32
+U16 = mybir.dt.uint16
+U8 = mybir.dt.uint8
+FP8X4 = mybir.dt.float8_e4m3fn_x4
+FP4X4 = mybir.dt.float4_e2m1fn_x4
+COPY = mybir.ActivationFunctionType.Copy
+ADD = mybir.AluOpType.add
+MULT = mybir.AluOpType.mult
+
+P = 128
+PACK = 4
+BLOCKS = E // P
+CHUNKS = T // P
+BANK = 512
+HALF = I // 2
+LIST_COLS = I // 16
+WINDOWS = 3
+REGION_A, REGION_B, REGION_C, REGION_D = 0, 1024, 9216, 11264
+
+
+def tile_attend_cachewrite_kernel(tc, emb_words, emb_scales, wv, old, retain, offs, offs2, out):
+    nc = tc.nc
+    with ExitStack() as ctx:
+        keep = ctx.enter_context(tc.tile_pool(name="keep", bufs=1))
+        shared = ctx.enter_context(tc.tile_pool(name="shared", bufs=1))
+        psum = ctx.enter_context(tc.psum_pool(name="psum", bufs=1))
+
+        def tenant(region, shape, dtype, name):
+            return shared.tile(shape, dtype, name=name, offset=region, align_bytes=64)
+
+        banks = [psum.tile([P, BANK], F32, name="bank%d" % n) for n in range(6)]
+
+        emb_list = keep.tile([P, LIST_COLS], U16, name="emb_list")
+        place_list = keep.tile([P, LIST_COLS], U16, name="place_list")
+        words = keep.tile([P, U], U16, name="words", align_bytes=64)
+        scales = tenant(REGION_B, [P, U], U8, "scales")
+        listed_words = tenant(REGION_A, [P, I], U16, "listed_words")
+        listed_scales = keep.tile([P, I], U8, name="listed_scales", align_bytes=64)
+        wv_raw = [keep.tile([P, PACK, P], F32, name="wv_raw%d" % b) for b in range(BLOCKS - 1)]
+        wv_raw.append(tenant(REGION_D, [P, PACK, P], F32, "wv_raw_last"))
+        first_bf = tenant(REGION_A, [P, P * PACK], BF16, "first_bf")
+        rest_bf = tenant(REGION_B, [P, (E - P) * PACK], BF16, "rest_bf")
+        first_codes = tenant(REGION_B, [P, P], U32, "first_codes")
+        rest_codes = tenant(REGION_C, [P, E - P], U32, "rest_codes")
+        second_half = tenant(REGION_D, [P, HALF], F32, "second_half")
+        kept_first = tenant(REGION_B, [P, 2 * T], F32, "kept_first")
+        wv_scales = keep.tile([P, E], U8, name="wv_scales", align_bytes=64)
+        old_sb = [keep.tile([P, T], F32, name="old_sb%d" % b) for b in range(BLOCKS)]
+        values = {b: keep.tile([P, I], F32, name="values%d" % b) for b in range(1, BLOCKS)}
+        first_half = tenant(REGION_C, [P, HALF], F32, "first_half")
+        windows = [keep.tile([P, T], F32, name="window%d" % w) for w in range(WINDOWS)]
+        turned = keep.tile([P, CHUNKS, 2, P], F32, name="turned")
+        kept_last = keep.tile([P, T], F32, name="kept_last")
+        retain_all = keep.tile([P, T], F32, name="retain_all")
+        result = [keep.tile([P, T], F32, name="result%d" % b) for b in range(BLOCKS)]
+        ident = keep.tile([P, P], F32, name="ident")
+        retain_rows = tenant(REGION_A, [P, P], F32, "retain_rows")
+        retain_cols = keep.tile([P, CHUNKS], F32, name="retain_cols")
+
+        nc.gpsimd.memset(retain_rows[:], 0.0)
+        nc.gpsimd.memset(scales[:].bitcast(I32), 0)
+        for w in range(WINDOWS):
+            nc.vector.memset(windows[w][:], 0.0)
+        make_identity(nc, ident[:])
+
+        def load_wv(b):
+            nc.sync.dma_start(out=wv_raw[b][:], in_=wv[:, b * P : (b + 1) * P].rearrange("(p j) e -> p j e", j=PACK))
+
+        def load_old(b):
+            nc.sync.dma_start(out=old_sb[b][:], in_=old[b * P : (b + 1) * P, :])
+
+        nc.sync.dma_start(emb_list[:], offs)
+        nc.sync.dma_start(out=retain_rows[0:CHUNKS, :], in_=retain.rearrange("o (c p) -> (o c) p", p=P))
+        load_wv(0)
+        scale_rows = emb_scales[0].rearrange("(q r) c -> r q c", r=4)
+        for r in range(4):
+            nc.sync.dma_start(out=scales[r:P:32, :].bitcast(I32), in_=scale_rows[r].bitcast(I32))
+        nc.sync.dma_start(out=words[:].bitcast(I32), in_=emb_words[0].bitcast(I32))
+        nc.sync.dma_start(place_list[:], offs2)
+        for b in range(1, BLOCKS):
+            load_wv(b)
+        for b in range(BLOCKS):
+            load_old(b)
+
+        def interleave(b):
+            dst = first_bf[:] if b == 0 else rest_bf[:, (b - 1) * P * PACK : b * P * PACK]
+            nc.scalar.activation(
+                out=dst.rearrange("p (c i j) -> p c j i", i=4, j=PACK),
+                in_=wv_raw[b][:].rearrange("p j (c i) -> p c j i", i=4),
+                func=COPY,
+            )
+
+        def project(b, lo, hi, acc):
+            nc.tensor.matmul_mx(
+                out=acc[:, 0 : hi - lo],
+                lhsT=wv_codes[b].bitcast(FP8X4),
+                lhsT_scale=wv_scales[:, b * P : (b + 1) * P],
+                rhs=listed_words[:, lo:hi].bitcast(FP4X4),
+                rhs_scale=listed_scales[:, lo:hi],
+                start=True,
+                stop=True,
+            )
+
+        def scatter(b, lo, hi, src):
+            nc.vector.tensor_copy(windows[b % WINDOWS][:].indirect(place_list[:, lo // 16 : hi // 16]), src)
+
+        def retain_turned(pair):
+            for q in range(CHUNKS // 2):
+                bank = banks[1 - q % 2][:].rearrange("p (c s e) -> p c s e", c=2, s=2)
+                for c in range(2):
+                    col = (2 * q + c) * P
+                    for s, b in enumerate(pair):
+                        nc.tensor.transpose(bank[:, c, s, :], old_sb[b][:, col : col + P], ident[:])
+                for c in range(2):
+                    chunk = 2 * q + c
+                    nc.scalar.activation(out=turned[:, chunk], in_=bank[:, c], func=COPY, scale=retain_cols[:, chunk : chunk + 1])
+            backs = {}
+            for s, b in enumerate(pair):
+                for h in range(T // BANK):
+                    back = banks[2 + 2 * s + h]
+                    for c in range(4):
+                        nc.tensor.transpose(back[:, c * P : (c + 1) * P], turned[:, 4 * h + c, s, :], ident[:])
+                    backs[b, h] = back
+            return backs
+
+        def retain_plain(b):
+            for h in range(T // BANK):
+                cols = slice(h * BANK, (h + 1) * BANK)
+                nc.gpsimd.tensor_tensor(kept[b][:, cols], old_sb[b][:, cols], retain_all[:, cols], MULT)
+
+        def finish(b):
+            for h in range(T // BANK):
+                cols = slice(h * BANK, (h + 1) * BANK)
+                nc.gpsimd.tensor_tensor(result[b][:, cols], kept[b][:, cols], windows[b % WINDOWS][:, cols], ADD)
+                nc.sync.dma_start(out=out[b * P : (b + 1) * P, cols], in_=result[b][:, cols])
+
+        retain_bank = banks[2]
+        nc.tensor.transpose(retain_bank[:, 0:P], retain_rows[:], ident[:])
+        nc.scalar.copy(out=retain_cols[:], in_=retain_bank[:, 0:CHUNKS])
+        interleave(0)
+        for h in range(T // BANK):
+            spread = banks[h]
+            for c in range(4):
+                chunk = 4 * h + c
+                nc.tensor.transpose(spread[:, c * P : (c + 1) * P], retain_cols[:, chunk : chunk + 1].to_broadcast([P, P]), ident[:])
+            nc.scalar.copy(out=retain_all[:, h * BANK : (h + 1) * BANK], in_=spread[:])
+
+        nc.vector.tensor_copy(listed_scales[:], scales[:].indirect(emb_list[:]))
+        nc.vector.quantize_mx(out=first_codes[:].bitcast(FP8X4), scales=wv_scales[:, 0:P], in_=first_bf[:])
+        wv_codes = {0: first_codes[:]}
+        for lo in (0, HALF):
+            nc.vector.tensor_copy(listed_words[:, lo : lo + HALF], words[:].indirect(emb_list[:, lo // 16 : (lo + HALF) // 16]))
+        project(0, 0, HALF, banks[0])
+        nc.scalar.copy(out=first_half[:], in_=banks[0][:, 0:HALF])
+        scatter(0, 0, HALF, first_half[:])
+        project(0, HALF, I, banks[1])
+        for b in range(1, BLOCKS):
+            interleave(b)
+        nc.scalar.copy(out=second_half[:], in_=banks[1][:, 0:HALF])
+        for lo, hi in ((0, P), (P, E - P)):
+            nc.vector.quantize_mx(
+                out=rest_codes[:, lo:hi].bitcast(FP8X4), scales=wv_scales[:, P + lo : P + hi], in_=rest_bf[:, lo * PACK : hi * PACK]
+            )
+        scatter(0, HALF, I, second_half[:])
+        for b in range(1, BLOCKS):
+            wv_codes[b] = rest_codes[:, (b - 1) * P : b * P]
+            project(b, 0, I, banks[(b - 1) % 2])
+            nc.scalar.copy(out=values[b][:], in_=banks[(b - 1) % 2][:])
+
+        kept = {0: kept_first[:, 0:T], 1: kept_first[:, T : 2 * T], 2: kept_last[:]}
+        retain_plain(0)
+        retain_plain(1)
+        backs = retain_turned((2, 3))
+        for h in range(T // BANK):
+            nc.scalar.copy(out=kept[2][:, h * BANK : (h + 1) * BANK], in_=backs[2, h][:])
+        for b in range(1, BLOCKS):
+            scatter(b, 0, I, values[b][:])
+            finish(b - 1)
+        last = BLOCKS - 1
+        for h in range(T // BANK):
+            cols = slice(h * BANK, (h + 1) * BANK)
+            nc.vector.tensor_tensor(result[last][:, cols], backs[last, h][:], windows[last % WINDOWS][:, cols], ADD)
+            queue = nc.sync if h == 0 else nc.scalar
+            queue.dma_start(out=out[last * P :, cols], in_=result[last][:, cols])

@@ -20,13 +20,26 @@ MULT = mybir.AluOpType.mult
 
 P = 128
 PACK = 4
+LINE = 4
 BLOCKS = E // P
 CHUNKS = T // P
 BANK = 512
 HALF = I // 2
-LIST_COLS = I // 16
+GROUP = 16
 WINDOWS = 3
-REGION_A, REGION_B, REGION_C, REGION_D = 0, 1024, 9216, 11264
+ALIGN = 64
+
+AT_KEPT0 = 0
+AT_BF0 = 4 * T
+AT_BF1 = AT_BF0 + ALIGN - 2 * P * PACK
+AT_SCALES0 = AT_BF0 + ALIGN
+AT_WORDS0 = AT_SCALES0 + HALF
+AT_WORDS1 = AT_WORDS0 + 2 * HALF
+AT_CODES0 = AT_WORDS1 + 2 * HALF
+AT_RAW1 = AT_CODES0 + 4 * T
+AT_RAW3 = AT_RAW1 + 4 * P * PACK
+AT_POOL = AT_RAW3 + 4 * P * PACK
+AT_RAW0 = AT_POOL + 2 * U
 
 
 def tile_attend_cachewrite_kernel(tc, emb_words, emb_scales, wv, old, retain, offs, offs2, out):
@@ -36,42 +49,52 @@ def tile_attend_cachewrite_kernel(tc, emb_words, emb_scales, wv, old, retain, of
         shared = ctx.enter_context(tc.tile_pool(name="shared", bufs=1))
         psum = ctx.enter_context(tc.psum_pool(name="psum", bufs=1))
 
-        def tenant(region, shape, dtype, name):
-            return shared.tile(shape, dtype, name=name, offset=region, align_bytes=64)
+        def placed(offset, shape, dtype, name):
+            return shared.tile(shape, dtype, name=name, offset=offset, align_bytes=ALIGN)
 
         banks = [psum.tile([P, BANK], F32, name="bank%d" % n) for n in range(6)]
 
-        emb_list = keep.tile([P, LIST_COLS], U16, name="emb_list")
-        place_list = keep.tile([P, LIST_COLS], U16, name="place_list")
-        words = keep.tile([P, U], U16, name="words", align_bytes=64)
-        scales = tenant(REGION_B, [P, U], U8, "scales")
-        listed_words = tenant(REGION_A, [P, I], U16, "listed_words")
-        listed_scales = keep.tile([P, I], U8, name="listed_scales", align_bytes=64)
-        wv_raw = [keep.tile([P, PACK, P], F32, name="wv_raw%d" % b) for b in range(BLOCKS - 1)]
-        wv_raw.append(tenant(REGION_D, [P, PACK, P], F32, "wv_raw_last"))
-        first_bf = tenant(REGION_A, [P, P * PACK], BF16, "first_bf")
-        rest_bf = tenant(REGION_B, [P, (E - P) * PACK], BF16, "rest_bf")
-        first_codes = tenant(REGION_B, [P, P], U32, "first_codes")
-        rest_codes = tenant(REGION_C, [P, E - P], U32, "rest_codes")
-        second_half = tenant(REGION_D, [P, HALF], F32, "second_half")
-        kept_first = tenant(REGION_B, [P, 2 * T], F32, "kept_first")
-        wv_scales = keep.tile([P, E], U8, name="wv_scales", align_bytes=64)
-        old_sb = [keep.tile([P, T], F32, name="old_sb%d" % b) for b in range(BLOCKS)]
-        values = {b: keep.tile([P, I], F32, name="values%d" % b) for b in range(1, BLOCKS)}
-        first_half = tenant(REGION_C, [P, HALF], F32, "first_half")
+        emb_list = keep.tile([P, I // GROUP], U16, name="emb_list")
+        place_list = keep.tile([P, I // GROUP], U16, name="place_list")
+        pool_words = placed(AT_POOL, [P, U], U16, "pool_words")
+        pool_scales = keep.tile([P, U], U8, name="pool_scales", align_bytes=ALIGN)
+        listed_words = [placed(AT_WORDS0, [P, HALF], U16, "listed_words0"), placed(AT_WORDS1, [P, HALF], U16, "listed_words1")]
+        listed_scales = [placed(AT_SCALES0, [P, HALF], U8, "listed_scales0"), placed(AT_POOL, [P, HALF], U8, "listed_scales1")]
+
+        wv_raw = [
+            placed(AT_RAW0, [P, PACK, P], F32, "wv_raw0"),
+            placed(AT_RAW1, [P, PACK, P], F32, "wv_raw1"),
+            keep.tile([P, PACK, P], F32, name="wv_raw2"),
+            placed(AT_RAW3, [P, PACK, P], F32, "wv_raw3"),
+        ]
+        wv_bf0 = placed(AT_BF0, [P, P * PACK], BF16, "wv_bf0")
+        wv_bf1 = placed(AT_BF1, [P, P * PACK], BF16, "wv_bf1")
+        wv_bf23 = placed(AT_CODES0, [P, 2 * P * PACK], BF16, "wv_bf23")
+        wv_bf = [wv_bf0[:], wv_bf1[:], wv_bf23[:, 0 : P * PACK], wv_bf23[:, P * PACK :]]
+        codes0 = placed(AT_CODES0, [P, P], U32, "codes0")
+        codes123 = keep.tile([P, E - P], U32, name="codes123", align_bytes=ALIGN)
+        wv_codes = [codes0[:]] + [codes123[:, n * P : (n + 1) * P] for n in range(BLOCKS - 1)]
+        wv_scales = keep.tile([P, E], U8, name="wv_scales", align_bytes=ALIGN)
+
+        values0 = [placed(AT_RAW1, [P, HALF], F32, "values0a"), keep.tile([P, HALF], F32, name="values0b")]
+        values = {1: placed(AT_RAW3, [P, I], F32, "values1")}
+        for b in (2, 3):
+            values[b] = keep.tile([P, I], F32, name="values%d" % b)
         windows = [keep.tile([P, T], F32, name="window%d" % w) for w in range(WINDOWS)]
+
+        old_sb = [keep.tile([P, T], F32, name="old_sb%d" % b) for b in range(BLOCKS)]
+        retain_rows = placed(AT_BF0, [P, P], F32, "retain_rows")
+        retain_cols = keep.tile([P, CHUNKS], F32, name="retain_cols")
+        retain_all = placed(AT_RAW0, [P, T], F32, "retain_all")
         turned = keep.tile([P, CHUNKS, 2, P], F32, name="turned")
-        kept_last = keep.tile([P, T], F32, name="kept_last")
-        retain_all = keep.tile([P, T], F32, name="retain_all")
+        kept = [placed(AT_KEPT0, [P, T], F32, "kept0"), placed(AT_CODES0, [P, T], F32, "kept1"), keep.tile([P, T], F32, name="kept2")]
         result = [keep.tile([P, T], F32, name="result%d" % b) for b in range(BLOCKS)]
         ident = keep.tile([P, P], F32, name="ident")
-        retain_rows = tenant(REGION_A, [P, P], F32, "retain_rows")
-        retain_cols = keep.tile([P, CHUNKS], F32, name="retain_cols")
 
         nc.gpsimd.memset(retain_rows[:], 0.0)
-        nc.gpsimd.memset(scales[:].bitcast(I32), 0)
-        for w in range(WINDOWS):
-            nc.vector.memset(windows[w][:], 0.0)
+        nc.gpsimd.memset(pool_scales[:].bitcast(I32), 0)
+        for window in windows:
+            nc.vector.memset(window[:], 0.0)
         make_identity(nc, ident[:])
 
         def load_wv(b):
@@ -83,113 +106,111 @@ def tile_attend_cachewrite_kernel(tc, emb_words, emb_scales, wv, old, retain, of
         nc.sync.dma_start(emb_list[:], offs)
         nc.sync.dma_start(out=retain_rows[0:CHUNKS, :], in_=retain.rearrange("o (c p) -> (o c) p", p=P))
         load_wv(0)
-        scale_rows = emb_scales[0].rearrange("(q r) c -> r q c", r=4)
+        scale_rows = emb_scales[0].rearrange("(q r) u -> r q u", r=4)
         for r in range(4):
-            nc.sync.dma_start(out=scales[r:P:32, :].bitcast(I32), in_=scale_rows[r].bitcast(I32))
-        nc.sync.dma_start(out=words[:].bitcast(I32), in_=emb_words[0].bitcast(I32))
+            nc.sync.dma_start(out=pool_scales[r:P:32, :].bitcast(I32), in_=scale_rows[r].bitcast(I32))
+        nc.sync.dma_start(out=pool_words[:].bitcast(I32), in_=emb_words[0].bitcast(I32))
         nc.sync.dma_start(place_list[:], offs2)
+        load_wv(1)
+        load_old(0)
+        load_wv(2)
+        load_wv(3)
         for b in range(1, BLOCKS):
-            load_wv(b)
-        for b in range(BLOCKS):
             load_old(b)
 
-        def interleave(b):
-            dst = first_bf[:] if b == 0 else rest_bf[:, (b - 1) * P * PACK : b * P * PACK]
+        def cast(b):
             nc.scalar.activation(
-                out=dst.rearrange("p (c i j) -> p c j i", i=4, j=PACK),
-                in_=wv_raw[b][:].rearrange("p j (c i) -> p c j i", i=4),
+                out=wv_bf[b].rearrange("p (c i j) -> p c j i", i=LINE, j=PACK),
+                in_=wv_raw[b][:].rearrange("p j (c i) -> p c j i", i=LINE),
                 func=COPY,
             )
 
-        def project(b, lo, hi, acc):
+        def gather(listed, pool, half):
+            nc.vector.tensor_copy(listed[half][:], pool[:].indirect(emb_list[:, half * HALF // GROUP : (half + 1) * HALF // GROUP]))
+
+        def project(b, half, acc):
             nc.tensor.matmul_mx(
-                out=acc[:, 0 : hi - lo],
+                out=acc,
                 lhsT=wv_codes[b].bitcast(FP8X4),
                 lhsT_scale=wv_scales[:, b * P : (b + 1) * P],
-                rhs=listed_words[:, lo:hi].bitcast(FP4X4),
-                rhs_scale=listed_scales[:, lo:hi],
+                rhs=listed_words[half][:].bitcast(FP4X4),
+                rhs_scale=listed_scales[half][:],
                 start=True,
                 stop=True,
             )
 
+        def project_block(b):
+            bank = banks[(b - 1) % 2]
+            for half in range(2):
+                project(b, half, bank[:, half * HALF : (half + 1) * HALF])
+            nc.scalar.copy(out=values[b][:], in_=bank[:])
+
         def scatter(b, lo, hi, src):
-            nc.vector.tensor_copy(windows[b % WINDOWS][:].indirect(place_list[:, lo // 16 : hi // 16]), src)
+            nc.vector.tensor_copy(windows[b % WINDOWS][:].indirect(place_list[:, lo // GROUP : hi // GROUP]), src)
 
-        def retain_turned(pair):
-            for q in range(CHUNKS // 2):
-                bank = banks[1 - q % 2][:].rearrange("p (c s e) -> p c s e", c=2, s=2)
-                for c in range(2):
-                    col = (2 * q + c) * P
-                    for s, b in enumerate(pair):
-                        nc.tensor.transpose(bank[:, c, s, :], old_sb[b][:, col : col + P], ident[:])
-                for c in range(2):
-                    chunk = 2 * q + c
-                    nc.scalar.activation(out=turned[:, chunk], in_=bank[:, c], func=COPY, scale=retain_cols[:, chunk : chunk + 1])
-            backs = {}
-            for s, b in enumerate(pair):
-                for h in range(T // BANK):
-                    back = banks[2 + 2 * s + h]
-                    for c in range(4):
-                        nc.tensor.transpose(back[:, c * P : (c + 1) * P], turned[:, 4 * h + c, s, :], ident[:])
-                    backs[b, h] = back
-            return backs
-
-        def retain_plain(b):
-            for h in range(T // BANK):
-                cols = slice(h * BANK, (h + 1) * BANK)
-                nc.gpsimd.tensor_tensor(kept[b][:, cols], old_sb[b][:, cols], retain_all[:, cols], MULT)
-
-        def finish(b):
-            for h in range(T // BANK):
-                cols = slice(h * BANK, (h + 1) * BANK)
+        def add_and_store(b, pieces):
+            for n in range(pieces):
+                cols = slice(n * T // pieces, (n + 1) * T // pieces)
                 nc.gpsimd.tensor_tensor(result[b][:, cols], kept[b][:, cols], windows[b % WINDOWS][:, cols], ADD)
                 nc.sync.dma_start(out=out[b * P : (b + 1) * P, cols], in_=result[b][:, cols])
 
-        retain_bank = banks[2]
-        nc.tensor.transpose(retain_bank[:, 0:P], retain_rows[:], ident[:])
-        nc.scalar.copy(out=retain_cols[:], in_=retain_bank[:, 0:CHUNKS])
-        interleave(0)
+        nc.tensor.transpose(banks[2][:, 0:P], retain_rows[:], ident[:])
+        nc.scalar.copy(out=retain_cols[:], in_=banks[2][:, 0:CHUNKS])
+        cast(0)
         for h in range(T // BANK):
-            spread = banks[h]
-            for c in range(4):
-                chunk = 4 * h + c
-                nc.tensor.transpose(spread[:, c * P : (c + 1) * P], retain_cols[:, chunk : chunk + 1].to_broadcast([P, P]), ident[:])
-            nc.scalar.copy(out=retain_all[:, h * BANK : (h + 1) * BANK], in_=spread[:])
+            for c in range(BANK // P):
+                chunk = h * BANK // P + c
+                nc.tensor.transpose(banks[h][:, c * P : (c + 1) * P], retain_cols[:, chunk : chunk + 1].to_broadcast([P, P]), ident[:])
+            nc.scalar.copy(out=retain_all[:, h * BANK : (h + 1) * BANK], in_=banks[h][:])
 
-        nc.vector.tensor_copy(listed_scales[:], scales[:].indirect(emb_list[:]))
-        nc.vector.quantize_mx(out=first_codes[:].bitcast(FP8X4), scales=wv_scales[:, 0:P], in_=first_bf[:])
-        wv_codes = {0: first_codes[:]}
-        for lo in (0, HALF):
-            nc.vector.tensor_copy(listed_words[:, lo : lo + HALF], words[:].indirect(emb_list[:, lo // 16 : (lo + HALF) // 16]))
-        project(0, 0, HALF, banks[0])
-        nc.scalar.copy(out=first_half[:], in_=banks[0][:, 0:HALF])
-        scatter(0, 0, HALF, first_half[:])
-        project(0, HALF, I, banks[1])
-        for b in range(1, BLOCKS):
-            interleave(b)
-        nc.scalar.copy(out=second_half[:], in_=banks[1][:, 0:HALF])
-        for lo, hi in ((0, P), (P, E - P)):
-            nc.vector.quantize_mx(
-                out=rest_codes[:, lo:hi].bitcast(FP8X4), scales=wv_scales[:, P + lo : P + hi], in_=rest_bf[:, lo * PACK : hi * PACK]
-            )
-        scatter(0, HALF, I, second_half[:])
-        for b in range(1, BLOCKS):
-            wv_codes[b] = rest_codes[:, (b - 1) * P : b * P]
-            project(b, 0, I, banks[(b - 1) % 2])
-            nc.scalar.copy(out=values[b][:], in_=banks[(b - 1) % 2][:])
+        nc.vector.quantize_mx(out=codes0[:].bitcast(FP8X4), scales=wv_scales[:, 0:P], in_=wv_bf0[:])
+        gather(listed_scales, pool_scales, 0)
+        gather(listed_words, pool_words, 0)
+        gather(listed_words, pool_words, 1)
+        gather(listed_scales, pool_scales, 1)
+        project(0, 0, banks[0][:, 0:HALF])
+        cast(1)
+        nc.vector.quantize_mx(out=wv_codes[1].bitcast(FP8X4), scales=wv_scales[:, P : 2 * P], in_=wv_bf1[:])
+        nc.scalar.copy(out=values0[0][:], in_=banks[0][:, 0:HALF])
+        scatter(0, 0, HALF, values0[0][:])
+        project(0, 1, banks[1][:, 0:HALF])
+        nc.scalar.copy(out=values0[1][:], in_=banks[1][:, 0:HALF])
+        scatter(0, HALF, I, values0[1][:])
+        nc.gpsimd.tensor_tensor(kept[0][:], old_sb[0][:], retain_all[:], MULT)
 
-        kept = {0: kept_first[:, 0:T], 1: kept_first[:, T : 2 * T], 2: kept_last[:]}
-        retain_plain(0)
-        retain_plain(1)
-        backs = retain_turned((2, 3))
+        cast(2)
+        cast(3)
+        nc.vector.quantize_mx(out=codes123[:, P:].bitcast(FP8X4), scales=wv_scales[:, 2 * P :], in_=wv_bf23[:])
+        for b in range(1, BLOCKS):
+            project_block(b)
+        add_and_store(0, 1)
+        nc.gpsimd.tensor_tensor(kept[1][:], old_sb[1][:], retain_all[:], MULT)
+
+        for pair in range(CHUNKS // 2):
+            bank = banks[1 - pair % 2][:].rearrange("p (c s e) -> p c s e", c=2, s=2)
+            for c in range(2):
+                col = (2 * pair + c) * P
+                for s in range(2):
+                    nc.tensor.transpose(bank[:, c, s, :], old_sb[2 + s][:, col : col + P], ident[:])
+            for c in range(2):
+                chunk = 2 * pair + c
+                nc.scalar.activation(out=turned[:, chunk], in_=bank[:, c], func=COPY, scale=retain_cols[:, chunk : chunk + 1])
+        for s in range(2):
+            for chunk in range(CHUNKS):
+                h, c = divmod(chunk, BANK // P)
+                nc.tensor.transpose(banks[2 + 2 * s + h][:, c * P : (c + 1) * P], turned[:, chunk, s, :], ident[:])
         for h in range(T // BANK):
-            nc.scalar.copy(out=kept[2][:, h * BANK : (h + 1) * BANK], in_=backs[2, h][:])
-        for b in range(1, BLOCKS):
-            scatter(b, 0, I, values[b][:])
-            finish(b - 1)
+            nc.scalar.copy(out=kept[2][:, h * BANK : (h + 1) * BANK], in_=banks[2 + h][:])
+
+        scatter(1, 0, I, values[1][:])
+        add_and_store(1, 1)
+        scatter(2, 0, I, values[2][:])
+        add_and_store(2, 2)
         last = BLOCKS - 1
-        for h in range(T // BANK):
-            cols = slice(h * BANK, (h + 1) * BANK)
-            nc.vector.tensor_tensor(result[last][:, cols], backs[last, h][:], windows[last % WINDOWS][:, cols], ADD)
-            queue = nc.sync if h == 0 else nc.scalar
-            queue.dma_start(out=out[last * P :, cols], in_=result[last][:, cols])
+        scatter(last, 0, I, values[last][:])
+        for lo, hi, queue in ((0, BANK, nc.sync), (BANK, T - T // 4, nc.scalar), (T - T // 4, T, nc.sync)):
+            h = lo // BANK
+            nc.vector.tensor_tensor(
+                result[last][:, lo:hi], banks[4 + h][:, lo - h * BANK : hi - h * BANK], windows[last % WINDOWS][:, lo:hi], ADD
+            )
+            queue.dma_start(out=out[last * P :, lo:hi], in_=result[last][:, lo:hi])

@@ -32,14 +32,11 @@ ALIGN = 64
 AT_KEPT0 = 0
 AT_BF0 = 4 * T
 AT_BF1 = AT_BF0 + ALIGN - 2 * P * PACK
-AT_SCALES0 = AT_BF0 + ALIGN
-AT_WORDS0 = AT_SCALES0 + HALF
-AT_WORDS1 = AT_WORDS0 + 2 * HALF
-AT_CODES0 = AT_WORDS1 + 2 * HALF
+AT_WORDS = AT_BF0 + ALIGN
+AT_CODES0 = AT_WORDS + 2 * I
 AT_RAW1 = AT_CODES0 + 4 * T
 AT_RAW3 = AT_RAW1 + 4 * P * PACK
-AT_POOL = AT_RAW3 + 4 * P * PACK
-AT_RAW0 = AT_POOL + 2 * U
+AT_RAW0 = AT_RAW3 + 4 * P * PACK
 
 
 def tile_attend_cachewrite_kernel(tc, emb_words, emb_scales, wv, old, retain, offs, offs2, out):
@@ -56,10 +53,10 @@ def tile_attend_cachewrite_kernel(tc, emb_words, emb_scales, wv, old, retain, of
 
         emb_list = keep.tile([P, I // GROUP], U16, name="emb_list")
         place_list = keep.tile([P, I // GROUP], U16, name="place_list")
-        pool_words = placed(AT_POOL, [P, U], U16, "pool_words")
+        pool_words = keep.tile([P, U], U16, name="pool_words", align_bytes=ALIGN)
         pool_scales = keep.tile([P, U], U8, name="pool_scales", align_bytes=ALIGN)
-        listed_words = [placed(AT_WORDS0, [P, HALF], U16, "listed_words0"), placed(AT_WORDS1, [P, HALF], U16, "listed_words1")]
-        listed_scales = [placed(AT_SCALES0, [P, HALF], U8, "listed_scales0"), placed(AT_POOL, [P, HALF], U8, "listed_scales1")]
+        listed_scales = keep.tile([P, I], U8, name="listed_scales", align_bytes=ALIGN)
+        listed_words = placed(AT_WORDS, [P, I], U16, "listed_words")
 
         wv_raw = [
             placed(AT_RAW0, [P, PACK, P], F32, "wv_raw0"),
@@ -92,7 +89,7 @@ def tile_attend_cachewrite_kernel(tc, emb_words, emb_scales, wv, old, retain, of
         ident = keep.tile([P, P], F32, name="ident")
 
         nc.gpsimd.memset(retain_rows[:], 0.0)
-        nc.gpsimd.memset(pool_scales[:].bitcast(I32), 0)
+        nc.vector.memset(pool_scales[:].bitcast(I32), 0)
         for window in windows:
             nc.vector.memset(window[:], 0.0)
         make_identity(nc, ident[:])
@@ -105,10 +102,10 @@ def tile_attend_cachewrite_kernel(tc, emb_words, emb_scales, wv, old, retain, of
 
         nc.sync.dma_start(emb_list[:], offs)
         nc.sync.dma_start(out=retain_rows[0:CHUNKS, :], in_=retain.rearrange("o (c p) -> (o c) p", p=P))
-        load_wv(0)
         scale_rows = emb_scales[0].rearrange("(q r) u -> r q u", r=4)
         for r in range(4):
             nc.sync.dma_start(out=pool_scales[r:P:32, :].bitcast(I32), in_=scale_rows[r].bitcast(I32))
+        load_wv(0)
         nc.sync.dma_start(out=pool_words[:].bitcast(I32), in_=emb_words[0].bitcast(I32))
         nc.sync.dma_start(place_list[:], offs2)
         load_wv(1)
@@ -125,25 +122,17 @@ def tile_attend_cachewrite_kernel(tc, emb_words, emb_scales, wv, old, retain, of
                 func=COPY,
             )
 
-        def gather(listed, pool, half):
-            nc.vector.tensor_copy(listed[half][:], pool[:].indirect(emb_list[:, half * HALF // GROUP : (half + 1) * HALF // GROUP]))
-
-        def project(b, half, acc):
+        def project(b, lo, hi, bank, dst):
             nc.tensor.matmul_mx(
-                out=acc,
+                out=bank[:, 0 : hi - lo],
                 lhsT=wv_codes[b].bitcast(FP8X4),
                 lhsT_scale=wv_scales[:, b * P : (b + 1) * P],
-                rhs=listed_words[half][:].bitcast(FP4X4),
-                rhs_scale=listed_scales[half][:],
+                rhs=listed_words[:, lo:hi].bitcast(FP4X4),
+                rhs_scale=listed_scales[:, lo:hi],
                 start=True,
                 stop=True,
             )
-
-        def project_block(b):
-            bank = banks[(b - 1) % 2]
-            for half in range(2):
-                project(b, half, bank[:, half * HALF : (half + 1) * HALF])
-            nc.scalar.copy(out=values[b][:], in_=bank[:])
+            nc.scalar.copy(out=dst[:], in_=bank[:, 0 : hi - lo])
 
         def scatter(b, lo, hi, src):
             nc.vector.tensor_copy(windows[b % WINDOWS][:].indirect(place_list[:, lo // GROUP : hi // GROUP]), src)
@@ -163,26 +152,22 @@ def tile_attend_cachewrite_kernel(tc, emb_words, emb_scales, wv, old, retain, of
                 nc.tensor.transpose(banks[h][:, c * P : (c + 1) * P], retain_cols[:, chunk : chunk + 1].to_broadcast([P, P]), ident[:])
             nc.scalar.copy(out=retain_all[:, h * BANK : (h + 1) * BANK], in_=banks[h][:])
 
+        nc.vector.tensor_copy(listed_scales[:], pool_scales[:].indirect(emb_list[:]))
         nc.vector.quantize_mx(out=codes0[:].bitcast(FP8X4), scales=wv_scales[:, 0:P], in_=wv_bf0[:])
-        gather(listed_scales, pool_scales, 0)
-        gather(listed_words, pool_words, 0)
-        gather(listed_words, pool_words, 1)
-        gather(listed_scales, pool_scales, 1)
-        project(0, 0, banks[0][:, 0:HALF])
+        for lo in (0, HALF):
+            nc.vector.tensor_copy(listed_words[:, lo : lo + HALF], pool_words[:].indirect(emb_list[:, lo // GROUP : (lo + HALF) // GROUP]))
         cast(1)
         nc.vector.quantize_mx(out=wv_codes[1].bitcast(FP8X4), scales=wv_scales[:, P : 2 * P], in_=wv_bf1[:])
-        nc.scalar.copy(out=values0[0][:], in_=banks[0][:, 0:HALF])
-        scatter(0, 0, HALF, values0[0][:])
-        project(0, 1, banks[1][:, 0:HALF])
-        nc.scalar.copy(out=values0[1][:], in_=banks[1][:, 0:HALF])
-        scatter(0, HALF, I, values0[1][:])
+        for half in range(2):
+            project(0, half * HALF, (half + 1) * HALF, banks[half], values0[half])
+            scatter(0, half * HALF, (half + 1) * HALF, values0[half][:])
         nc.gpsimd.tensor_tensor(kept[0][:], old_sb[0][:], retain_all[:], MULT)
 
         cast(2)
         cast(3)
         nc.vector.quantize_mx(out=codes123[:, P:].bitcast(FP8X4), scales=wv_scales[:, 2 * P :], in_=wv_bf23[:])
         for b in range(1, BLOCKS):
-            project_block(b)
+            project(b, 0, I, banks[(b - 1) % 2], values[b])
         add_and_store(0, 1)
         nc.gpsimd.tensor_tensor(kept[1][:], old_sb[1][:], retain_all[:], MULT)
 

@@ -25,6 +25,7 @@ BLOCKS = E // P
 CHUNKS = T // P
 BANK = 512
 HALF = I // 2
+QUARTER = T // 4
 GROUP = 16
 WINDOWS = 3
 ALIGN = 64
@@ -85,6 +86,7 @@ def tile_attend_cachewrite_kernel(tc, emb_words, emb_scales, wv, old, retain, of
         retain_all = placed(AT_RAW0, [P, T], F32, "retain_all")
         turned = keep.tile([P, CHUNKS, 2, P], F32, name="turned")
         kept = [placed(AT_KEPT0, [P, T], F32, "kept0"), placed(AT_CODES0, [P, T], F32, "kept1"), keep.tile([P, T], F32, name="kept2")]
+        kept_end = keep.tile([P, QUARTER], F32, name="kept_end")
         result = [keep.tile([P, T], F32, name="result%d" % b) for b in range(BLOCKS)]
         ident = keep.tile([P, P], F32, name="ident")
 
@@ -186,6 +188,7 @@ def tile_attend_cachewrite_kernel(tc, emb_words, emb_scales, wv, old, retain, of
                 nc.tensor.transpose(banks[2 + 2 * s + h][:, c * P : (c + 1) * P], turned[:, chunk, s, :], ident[:])
         for h in range(T // BANK):
             nc.scalar.copy(out=kept[2][:, h * BANK : (h + 1) * BANK], in_=banks[2 + h][:])
+        nc.scalar.copy(out=kept_end[:], in_=banks[5][:, BANK - QUARTER :])
 
         scatter(1, 0, I, values[1][:])
         add_and_store(1, 1)
@@ -193,9 +196,13 @@ def tile_attend_cachewrite_kernel(tc, emb_words, emb_scales, wv, old, retain, of
         add_and_store(2, 2)
         last = BLOCKS - 1
         scatter(last, 0, I, values[last][:])
-        for lo, hi, queue in ((0, BANK, nc.sync), (BANK, T - T // 4, nc.scalar), (T - T // 4, T, nc.sync)):
-            h = lo // BANK
-            nc.vector.tensor_tensor(
-                result[last][:, lo:hi], banks[4 + h][:, lo - h * BANK : hi - h * BANK], windows[last % WINDOWS][:, lo:hi], ADD
-            )
-            queue.dma_start(out=out[last * P :, lo:hi], in_=result[last][:, lo:hi])
+        window = windows[last % WINDOWS]
+        for n in range(4):
+            cols = slice(n * QUARTER, (n + 1) * QUARTER)
+            if n < 3:
+                h, c = divmod(n * QUARTER, BANK)
+                nc.vector.tensor_tensor(result[last][:, cols], banks[4 + h][:, c : c + QUARTER], window[:, cols], ADD)
+            else:
+                nc.gpsimd.tensor_tensor(result[last][:, cols], kept_end[:], window[:, cols], ADD)
+            queue = nc.sync if n % 2 == 0 else nc.scalar
+            queue.dma_start(out=out[last * P :, cols], in_=result[last][:, cols])

@@ -29,15 +29,16 @@ QUARTER = T // 4
 GROUP = 16
 WINDOWS = 3
 ALIGN = 64
+KIB = 1024
 
-AT_KEPT0 = 0
-AT_BF0 = 4 * T
-AT_BF1 = AT_BF0 + ALIGN - 2 * P * PACK
-AT_WORDS = AT_BF0 + ALIGN
-AT_CODES0 = AT_WORDS + 2 * I
-AT_RAW1 = AT_CODES0 + 4 * T
-AT_RAW3 = AT_RAW1 + 4 * P * PACK
-AT_RAW0 = AT_RAW3 + 4 * P * PACK
+AT_RAW0 = 0
+AT_BF0 = 4 * KIB
+AT_BF1 = 8 * KIB
+AT_RAW3 = 12 * KIB
+AT_RAW1 = 14 * KIB
+AT_BF23 = 15 * KIB
+AT_CODES0 = 16 * KIB
+AT_WORDS = 19 * KIB
 
 
 def tile_attend_cachewrite_kernel(tc, emb_words, emb_scales, wv, old, retain, offs, offs2, out):
@@ -50,14 +51,14 @@ def tile_attend_cachewrite_kernel(tc, emb_words, emb_scales, wv, old, retain, of
         def placed(offset, shape, dtype, name):
             return shared.tile(shape, dtype, name=name, offset=offset, align_bytes=ALIGN)
 
-        banks = [psum.tile([P, BANK], F32, name="bank%d" % n) for n in range(6)]
+        banks = [psum.tile([P, BANK], F32, name="bank%d" % n) for n in range(8)]
 
         emb_list = keep.tile([P, I // GROUP], U16, name="emb_list")
         place_list = keep.tile([P, I // GROUP], U16, name="place_list")
-        pool_words = keep.tile([P, U], U16, name="pool_words", align_bytes=ALIGN)
+        pool_words = placed(AT_WORDS, [P, U], U16, "pool_words")
         pool_scales = keep.tile([P, U], U8, name="pool_scales", align_bytes=ALIGN)
-        listed_scales = keep.tile([P, I], U8, name="listed_scales", align_bytes=ALIGN)
-        listed_words = placed(AT_WORDS, [P, I], U16, "listed_words")
+        listed_words = keep.tile([P, I], U16, name="listed_words", align_bytes=ALIGN)
+        listed_scales = [keep.tile([P, HALF], U8, name="listed_scales0", align_bytes=ALIGN), placed(AT_WORDS, [P, HALF], U8, "listed_scales1")]
 
         wv_raw = [
             placed(AT_RAW0, [P, PACK, P], F32, "wv_raw0"),
@@ -67,54 +68,65 @@ def tile_attend_cachewrite_kernel(tc, emb_words, emb_scales, wv, old, retain, of
         ]
         wv_bf0 = placed(AT_BF0, [P, P * PACK], BF16, "wv_bf0")
         wv_bf1 = placed(AT_BF1, [P, P * PACK], BF16, "wv_bf1")
-        wv_bf23 = placed(AT_CODES0, [P, 2 * P * PACK], BF16, "wv_bf23")
+        wv_bf23 = placed(AT_BF23, [P, 2 * P * PACK], BF16, "wv_bf23")
         wv_bf = [wv_bf0[:], wv_bf1[:], wv_bf23[:, 0 : P * PACK], wv_bf23[:, P * PACK :]]
         codes0 = placed(AT_CODES0, [P, P], U32, "codes0")
         codes123 = keep.tile([P, E - P], U32, name="codes123", align_bytes=ALIGN)
         wv_codes = [codes0[:]] + [codes123[:, n * P : (n + 1) * P] for n in range(BLOCKS - 1)]
         wv_scales = keep.tile([P, E], U8, name="wv_scales", align_bytes=ALIGN)
 
-        values0 = [placed(AT_RAW1, [P, HALF], F32, "values0a"), keep.tile([P, HALF], F32, name="values0b")]
-        values = {1: placed(AT_RAW3, [P, I], F32, "values1")}
+        values = {
+            (0, 0): placed(AT_RAW1, [P, HALF], F32, "values0a"),
+            (1, 0): keep.tile([P, HALF], F32, name="values1a"),
+            (0, 1): keep.tile([P, HALF], F32, name="values0b"),
+            (1, 1): placed(AT_RAW3, [P, HALF], F32, "values1b"),
+        }
         for b in (2, 3):
             values[b] = keep.tile([P, I], F32, name="values%d" % b)
-        windows = [keep.tile([P, T], F32, name="window%d" % w) for w in range(WINDOWS)]
+        windows = [keep.tile([P, T], F32, name="window%d" % w) for w in range(WINDOWS - 1)]
+        windows.append(placed(AT_BF0, [P, T], F32, "window2"))
 
         old_sb = [keep.tile([P, T], F32, name="old_sb%d" % b) for b in range(BLOCKS)]
-        retain_rows = placed(AT_BF0, [P, P], F32, "retain_rows")
+        retain_rows = keep.tile([P, P], F32, name="retain_rows")
         retain_cols = keep.tile([P, CHUNKS], F32, name="retain_cols")
+        retain_quads = keep.tile([P, 2, 2 * LINE], F32, name="retain_quads")
         retain_all = placed(AT_RAW0, [P, T], F32, "retain_all")
-        turned = keep.tile([P, CHUNKS, 2, P], F32, name="turned")
-        kept = [placed(AT_KEPT0, [P, T], F32, "kept0"), placed(AT_CODES0, [P, T], F32, "kept1"), keep.tile([P, T], F32, name="kept2")]
+        retain_half = [retain_all[:, 0:BANK], retain_all[:, BANK:]]
+        turned = [keep.tile([P, CHUNKS, P], F32, name="turned%d" % s) for s in range(2)]
+        kept = [placed(AT_BF1, [P, T], F32, "kept0"), keep.tile([P, T], F32, name="kept1"), keep.tile([P, T], F32, name="kept2")]
         kept_end = keep.tile([P, QUARTER], F32, name="kept_end")
         result = [keep.tile([P, T], F32, name="result%d" % b) for b in range(BLOCKS)]
         ident = keep.tile([P, P], F32, name="ident")
 
-        nc.gpsimd.memset(retain_rows[:], 0.0)
         nc.vector.memset(pool_scales[:].bitcast(I32), 0)
-        for window in windows:
-            nc.vector.memset(window[:], 0.0)
         make_identity(nc, ident[:])
+        nc.gpsimd.memset(retain_rows[:], 0.0)
+        nc.vector.memset(windows[0][:, 0 : T // 2 + 1], 0.0)
+        nc.vector.memset(windows[0][:, T // 2 + 1 :], 0.0)
+        for h in range(T // BANK):
+            nc.gpsimd.memset(windows[1][:, h * BANK : (h + 1) * BANK], 0.0)
 
-        def load_wv(b):
-            nc.sync.dma_start(out=wv_raw[b][:], in_=wv[:, b * P : (b + 1) * P].rearrange("(p j) e -> p j e", j=PACK))
+        def load_wv(b, queue=nc.sync):
+            queue.dma_start(out=wv_raw[b][:], in_=wv[:, b * P : (b + 1) * P].rearrange("(p j) e -> p j e", j=PACK))
 
         def load_old(b):
             nc.sync.dma_start(out=old_sb[b][:], in_=old[b * P : (b + 1) * P, :])
 
+        load_wv(0, nc.scalar)
         nc.sync.dma_start(emb_list[:], offs)
-        nc.sync.dma_start(out=retain_rows[0:CHUNKS, :], in_=retain.rearrange("o (c p) -> (o c) p", p=P))
+        nc.scalar.dma_start(out=pool_words[:].bitcast(I32), in_=emb_words[0].bitcast(I32))
+        nc.sync.dma_start(out=retain_quads[:, :, 0:LINE], in_=retain.rearrange("o (h p c) -> (o p) h c", h=2, c=LINE))
         scale_rows = emb_scales[0].rearrange("(q r) u -> r q u", r=4)
         for r in range(4):
             nc.sync.dma_start(out=pool_scales[r:P:32, :].bitcast(I32), in_=scale_rows[r].bitcast(I32))
-        load_wv(0)
-        nc.sync.dma_start(out=pool_words[:].bitcast(I32), in_=emb_words[0].bitcast(I32))
-        nc.sync.dma_start(place_list[:], offs2)
         load_wv(1)
+        nc.sync.dma_start(place_list[:], offs2)
         load_old(0)
+        load_old(1)
         load_wv(2)
         load_wv(3)
-        for b in range(1, BLOCKS):
+        nc.sync.dma_start(out=retain_rows[0:CHUNKS, :], in_=retain.rearrange("o (c p) -> (o c) p", p=P))
+        for b in range(2, BLOCKS):
             load_old(b)
 
         def cast(b):
@@ -124,20 +136,29 @@ def tile_attend_cachewrite_kernel(tc, emb_words, emb_scales, wv, old, retain, of
                 func=COPY,
             )
 
-        def project(b, lo, hi, bank, dst):
+        def project(b, half, dst):
             nc.tensor.matmul_mx(
-                out=bank[:, 0 : hi - lo],
+                out=dst,
                 lhsT=wv_codes[b].bitcast(FP8X4),
                 lhsT_scale=wv_scales[:, b * P : (b + 1) * P],
-                rhs=listed_words[:, lo:hi].bitcast(FP4X4),
-                rhs_scale=listed_scales[:, lo:hi],
+                rhs=listed_words[:, half * HALF : (half + 1) * HALF].bitcast(FP4X4),
+                rhs_scale=listed_scales[half][:],
                 start=True,
                 stop=True,
             )
-            nc.scalar.copy(out=dst[:], in_=bank[:, 0 : hi - lo])
 
         def scatter(b, lo, hi, src):
             nc.vector.tensor_copy(windows[b % WINDOWS][:].indirect(place_list[:, lo // GROUP : hi // GROUP]), src)
+
+        def spread_retain(h, bank):
+            for c in range(LINE):
+                nc.tensor.transpose(bank[:, c * P : (c + 1) * P], retain_quads[:, h, c : c + 1].to_broadcast([P, P]), ident[:])
+            nc.scalar.copy(out=retain_half[h].rearrange("p (n c) -> p n c", c=LINE), in_=bank[:].rearrange("p (c n) -> p n c", c=LINE))
+
+        def multiply(b):
+            for h in range(T // BANK):
+                cols = slice(h * BANK, (h + 1) * BANK)
+                nc.gpsimd.tensor_tensor(kept[b][:, cols], old_sb[b][:, cols], retain_half[h], MULT)
 
         def add_and_store(b, pieces):
             for n in range(pieces):
@@ -145,53 +166,61 @@ def tile_attend_cachewrite_kernel(tc, emb_words, emb_scales, wv, old, retain, of
                 nc.gpsimd.tensor_tensor(result[b][:, cols], kept[b][:, cols], windows[b % WINDOWS][:, cols], ADD)
                 nc.sync.dma_start(out=out[b * P : (b + 1) * P, cols], in_=result[b][:, cols])
 
-        nc.tensor.transpose(banks[2][:, 0:P], retain_rows[:], ident[:])
-        nc.scalar.copy(out=retain_cols[:], in_=banks[2][:, 0:CHUNKS])
-        cast(0)
-        for h in range(T // BANK):
-            for c in range(BANK // P):
-                chunk = h * BANK // P + c
-                nc.tensor.transpose(banks[h][:, c * P : (c + 1) * P], retain_cols[:, chunk : chunk + 1].to_broadcast([P, P]), ident[:])
-            nc.scalar.copy(out=retain_all[:, h * BANK : (h + 1) * BANK], in_=banks[h][:])
+        def multiply_turned(b, there, back):
+            for h in range(T // BANK):
+                for c in range(BANK // P):
+                    col = h * BANK + c * P
+                    nc.tensor.transpose(there[h][:, c * P : (c + 1) * P], old_sb[b][:, col : col + P], ident[:])
+                for c in range(BANK // P):
+                    chunk = h * BANK // P + c
+                    nc.scalar.activation(out=turned[b % 2][:, chunk], in_=there[h][:, c * P : (c + 1) * P], func=COPY, scale=retain_cols[:, chunk : chunk + 1])
+            for chunk in range(CHUNKS):
+                h, c = divmod(chunk, BANK // P)
+                nc.tensor.transpose(back[h][:, c * P : (c + 1) * P], turned[b % 2][:, chunk], ident[:])
 
-        nc.vector.tensor_copy(listed_scales[:], pool_scales[:].indirect(emb_list[:]))
+        cast(0)
+        spread_retain(0, banks[0])
+        spread_retain(1, banks[1])
+
+        half_lists = [emb_list[:, 0 : HALF // GROUP], emb_list[:, HALF // GROUP :]]
+        nc.vector.tensor_copy(listed_scales[0][:], pool_scales[:].indirect(half_lists[0]))
         nc.vector.quantize_mx(out=codes0[:].bitcast(FP8X4), scales=wv_scales[:, 0:P], in_=wv_bf0[:])
-        for lo in (0, HALF):
-            nc.vector.tensor_copy(listed_words[:, lo : lo + HALF], pool_words[:].indirect(emb_list[:, lo // GROUP : (lo + HALF) // GROUP]))
+        nc.gpsimd.memset(windows[2][:], 0.0)
+        for half in range(2):
+            nc.vector.tensor_copy(listed_words[:, half * HALF : (half + 1) * HALF], pool_words[:].indirect(half_lists[half]))
+        nc.vector.tensor_copy(listed_scales[1][:], pool_scales[:].indirect(half_lists[1]))
         cast(1)
         nc.vector.quantize_mx(out=wv_codes[1].bitcast(FP8X4), scales=wv_scales[:, P : 2 * P], in_=wv_bf1[:])
-        for half in range(2):
-            project(0, half * HALF, (half + 1) * HALF, banks[half], values0[half])
-            scatter(0, half * HALF, (half + 1) * HALF, values0[half][:])
-        nc.gpsimd.tensor_tensor(kept[0][:], old_sb[0][:], retain_all[:], MULT)
 
+        def half_step(b, half, bank):
+            project(b, half, bank[:, 0:HALF])
+            nc.scalar.copy(out=values[b, half][:], in_=bank[:, 0:HALF])
+            scatter(b, half * HALF, (half + 1) * HALF, values[b, half][:])
+
+        half_step(0, 0, banks[0])
+        half_step(1, 0, banks[1])
+        half_step(0, 1, banks[1])
+        multiply(0)
+        multiply(1)
         cast(2)
         cast(3)
         nc.vector.quantize_mx(out=codes123[:, P:].bitcast(FP8X4), scales=wv_scales[:, 2 * P :], in_=wv_bf23[:])
-        for b in range(1, BLOCKS):
-            project(b, 0, I, banks[(b - 1) % 2], values[b])
+        half_step(1, 1, banks[0])
+        for b in (2, 3):
+            for half in range(2):
+                project(b, half, banks[b][:, half * HALF : (half + 1) * HALF])
+            nc.scalar.copy(out=values[b][:], in_=banks[b][:])
         add_and_store(0, 1)
-        nc.gpsimd.tensor_tensor(kept[1][:], old_sb[1][:], retain_all[:], MULT)
-
-        for pair in range(CHUNKS // 2):
-            bank = banks[1 - pair % 2][:].rearrange("p (c s e) -> p c s e", c=2, s=2)
-            for c in range(2):
-                col = (2 * pair + c) * P
-                for s in range(2):
-                    nc.tensor.transpose(bank[:, c, s, :], old_sb[2 + s][:, col : col + P], ident[:])
-            for c in range(2):
-                chunk = 2 * pair + c
-                nc.scalar.activation(out=turned[:, chunk], in_=bank[:, c], func=COPY, scale=retain_cols[:, chunk : chunk + 1])
-        for s in range(2):
-            for chunk in range(CHUNKS):
-                h, c = divmod(chunk, BANK // P)
-                nc.tensor.transpose(banks[2 + 2 * s + h][:, c * P : (c + 1) * P], turned[:, chunk, s, :], ident[:])
-        for h in range(T // BANK):
-            nc.scalar.copy(out=kept[2][:, h * BANK : (h + 1) * BANK], in_=banks[2 + h][:])
-        nc.scalar.copy(out=kept_end[:], in_=banks[5][:, BANK - QUARTER :])
-
-        scatter(1, 0, I, values[1][:])
         add_and_store(1, 1)
+
+        nc.tensor.transpose(banks[1][:, 0:P], retain_rows[:], ident[:])
+        nc.scalar.copy(out=retain_cols[:], in_=banks[1][:, 0:CHUNKS])
+        multiply_turned(2, [banks[1], banks[0]], banks[4:6])
+        for h in range(T // BANK):
+            nc.scalar.copy(out=kept[2][:, h * BANK : (h + 1) * BANK], in_=banks[4 + h][:])
+        multiply_turned(3, [banks[2], banks[3]], banks[6:8])
+        nc.scalar.copy(out=kept_end[:], in_=banks[7][:, BANK - QUARTER :])
+
         scatter(2, 0, I, values[2][:])
         add_and_store(2, 2)
         last = BLOCKS - 1
@@ -201,7 +230,7 @@ def tile_attend_cachewrite_kernel(tc, emb_words, emb_scales, wv, old, retain, of
             cols = slice(n * QUARTER, (n + 1) * QUARTER)
             if n < 3:
                 h, c = divmod(n * QUARTER, BANK)
-                nc.vector.tensor_tensor(result[last][:, cols], banks[4 + h][:, c : c + QUARTER], window[:, cols], ADD)
+                nc.vector.tensor_tensor(result[last][:, cols], banks[6 + h][:, c : c + QUARTER], window[:, cols], ADD)
             else:
                 nc.gpsimd.tensor_tensor(result[last][:, cols], kept_end[:], window[:, cols], ADD)
             queue = nc.sync if n % 2 == 0 else nc.scalar

@@ -31,14 +31,16 @@ WINDOWS = 3
 ALIGN = 64
 KIB = 1024
 
-AT_RAW0 = 0
-AT_BF0 = 4 * KIB
-AT_BF1 = 8 * KIB
+AT_BF0 = 5 * KIB
+AT_BF1 = AT_BF0 + ALIGN - KIB
+AT_KEPT0 = AT_BF1 + ALIGN - 4 * KIB
+AT_WINDOW2 = AT_BF0 + KIB - ALIGN
+AT_RAW0 = 19 * KIB
 AT_RAW3 = 12 * KIB
+AT_WORDS = 22 * KIB
 AT_RAW1 = 14 * KIB
 AT_BF23 = 15 * KIB
 AT_CODES0 = 16 * KIB
-AT_WORDS = 19 * KIB
 
 
 def tile_attend_cachewrite_kernel(tc, emb_words, emb_scales, wv, old, retain, offs, offs2, out):
@@ -57,7 +59,7 @@ def tile_attend_cachewrite_kernel(tc, emb_words, emb_scales, wv, old, retain, of
         place_list = keep.tile([P, I // GROUP], U16, name="place_list")
         pool_words = placed(AT_WORDS, [P, U], U16, "pool_words")
         pool_scales = keep.tile([P, U], U8, name="pool_scales", align_bytes=ALIGN)
-        listed_words = keep.tile([P, I], U16, name="listed_words", align_bytes=ALIGN)
+        listed_words = [keep.tile([P, HALF], U16, name="listed_words0", align_bytes=ALIGN), keep.tile([P, HALF], U16, name="listed_words1", align_bytes=ALIGN)]
         listed_scales = [keep.tile([P, HALF], U8, name="listed_scales0", align_bytes=ALIGN), placed(AT_WORDS, [P, HALF], U8, "listed_scales1")]
 
         wv_raw = [
@@ -84,16 +86,15 @@ def tile_attend_cachewrite_kernel(tc, emb_words, emb_scales, wv, old, retain, of
         for b in (2, 3):
             values[b] = keep.tile([P, I], F32, name="values%d" % b)
         windows = [keep.tile([P, T], F32, name="window%d" % w) for w in range(WINDOWS - 1)]
-        windows.append(placed(AT_BF0, [P, T], F32, "window2"))
+        windows.append(placed(AT_WINDOW2, [P, T], F32, "window2"))
 
         old_sb = [keep.tile([P, T], F32, name="old_sb%d" % b) for b in range(BLOCKS)]
         retain_rows = keep.tile([P, P], F32, name="retain_rows")
         retain_cols = keep.tile([P, CHUNKS], F32, name="retain_cols")
-        retain_quads = keep.tile([P, 2, 2 * LINE], F32, name="retain_quads")
-        retain_all = placed(AT_RAW0, [P, T], F32, "retain_all")
-        retain_half = [retain_all[:, 0:BANK], retain_all[:, BANK:]]
+        retain_quads = placed(AT_BF1 + 2 * ALIGN, [P, 2, 2 * LINE], F32, "retain_quads")
+        retain_half = [placed(AT_RAW0 - KIB, [P, BANK], F32, "retain_lo"), placed(AT_RAW0 + KIB, [P, BANK], F32, "retain_hi")]
         turned = [keep.tile([P, CHUNKS, P], F32, name="turned%d" % s) for s in range(2)]
-        kept = [placed(AT_BF1, [P, T], F32, "kept0"), keep.tile([P, T], F32, name="kept1"), keep.tile([P, T], F32, name="kept2")]
+        kept = [placed(AT_KEPT0, [P, T], F32, "kept0"), keep.tile([P, T], F32, name="kept1"), keep.tile([P, T], F32, name="kept2")]
         kept_end = keep.tile([P, QUARTER], F32, name="kept_end")
         result = [keep.tile([P, T], F32, name="result%d" % b) for b in range(BLOCKS)]
         ident = keep.tile([P, P], F32, name="ident")
@@ -101,10 +102,9 @@ def tile_attend_cachewrite_kernel(tc, emb_words, emb_scales, wv, old, retain, of
         nc.vector.memset(pool_scales[:].bitcast(I32), 0)
         make_identity(nc, ident[:])
         nc.gpsimd.memset(retain_rows[:], 0.0)
-        nc.vector.memset(windows[0][:, 0 : T // 2 + 1], 0.0)
-        nc.vector.memset(windows[0][:, T // 2 + 1 :], 0.0)
-        for h in range(T // BANK):
-            nc.gpsimd.memset(windows[1][:, h * BANK : (h + 1) * BANK], 0.0)
+        for window in windows[0:2]:
+            nc.vector.memset(window[:, 0 : T // 2 + 1], 0.0)
+            nc.vector.memset(window[:, T // 2 + 1 :], 0.0)
 
         def load_wv(b, queue=nc.sync):
             queue.dma_start(out=wv_raw[b][:], in_=wv[:, b * P : (b + 1) * P].rearrange("(p j) e -> p j e", j=PACK))
@@ -112,13 +112,13 @@ def tile_attend_cachewrite_kernel(tc, emb_words, emb_scales, wv, old, retain, of
         def load_old(b):
             nc.sync.dma_start(out=old_sb[b][:], in_=old[b * P : (b + 1) * P, :])
 
+        nc.sync.dma_start(out=retain_quads[:, :, 0:LINE], in_=retain.rearrange("o (h p c) -> (o p) h c", h=2, c=LINE))
         load_wv(0, nc.scalar)
         nc.sync.dma_start(emb_list[:], offs)
-        nc.scalar.dma_start(out=pool_words[:].bitcast(I32), in_=emb_words[0].bitcast(I32))
-        nc.sync.dma_start(out=retain_quads[:, :, 0:LINE], in_=retain.rearrange("o (h p c) -> (o p) h c", h=2, c=LINE))
         scale_rows = emb_scales[0].rearrange("(q r) u -> r q u", r=4)
         for r in range(4):
             nc.sync.dma_start(out=pool_scales[r:P:32, :].bitcast(I32), in_=scale_rows[r].bitcast(I32))
+        nc.sync.dma_start(out=pool_words[:].bitcast(I32), in_=emb_words[0].bitcast(I32))
         load_wv(1)
         nc.sync.dma_start(place_list[:], offs2)
         load_old(0)
@@ -141,7 +141,7 @@ def tile_attend_cachewrite_kernel(tc, emb_words, emb_scales, wv, old, retain, of
                 out=dst,
                 lhsT=wv_codes[b].bitcast(FP8X4),
                 lhsT_scale=wv_scales[:, b * P : (b + 1) * P],
-                rhs=listed_words[:, half * HALF : (half + 1) * HALF].bitcast(FP4X4),
+                rhs=listed_words[half][:].bitcast(FP4X4),
                 rhs_scale=listed_scales[half][:],
                 start=True,
                 stop=True,
@@ -153,12 +153,12 @@ def tile_attend_cachewrite_kernel(tc, emb_words, emb_scales, wv, old, retain, of
         def spread_retain(h, bank):
             for c in range(LINE):
                 nc.tensor.transpose(bank[:, c * P : (c + 1) * P], retain_quads[:, h, c : c + 1].to_broadcast([P, P]), ident[:])
-            nc.scalar.copy(out=retain_half[h].rearrange("p (n c) -> p n c", c=LINE), in_=bank[:].rearrange("p (c n) -> p n c", c=LINE))
+            nc.scalar.copy(out=retain_half[h][:].rearrange("p (n c) -> p n c", c=LINE), in_=bank[:].rearrange("p (c n) -> p n c", c=LINE))
 
         def multiply(b):
             for h in range(T // BANK):
                 cols = slice(h * BANK, (h + 1) * BANK)
-                nc.gpsimd.tensor_tensor(kept[b][:, cols], old_sb[b][:, cols], retain_half[h], MULT)
+                nc.gpsimd.tensor_tensor(kept[b][:, cols], old_sb[b][:, cols], retain_half[h][:], MULT)
 
         def add_and_store(b, pieces):
             for n in range(pieces):
@@ -187,7 +187,7 @@ def tile_attend_cachewrite_kernel(tc, emb_words, emb_scales, wv, old, retain, of
         nc.vector.quantize_mx(out=codes0[:].bitcast(FP8X4), scales=wv_scales[:, 0:P], in_=wv_bf0[:])
         nc.gpsimd.memset(windows[2][:], 0.0)
         for half in range(2):
-            nc.vector.tensor_copy(listed_words[:, half * HALF : (half + 1) * HALF], pool_words[:].indirect(half_lists[half]))
+            nc.vector.tensor_copy(listed_words[half][:], pool_words[:].indirect(half_lists[half]))
         nc.vector.tensor_copy(listed_scales[1][:], pool_scales[:].indirect(half_lists[1]))
         cast(1)
         nc.vector.quantize_mx(out=wv_codes[1].bitcast(FP8X4), scales=wv_scales[:, P : 2 * P], in_=wv_bf1[:])

@@ -34,7 +34,6 @@ KIB = 1024
 AT_BF0 = 5 * KIB
 AT_BF1 = AT_BF0 + ALIGN - KIB
 AT_KEPT0 = AT_BF1 + ALIGN - 4 * KIB
-AT_WINDOW2 = AT_BF0 + KIB - ALIGN
 AT_RAW0 = 19 * KIB
 AT_RAW3 = 12 * KIB
 AT_WORDS = 22 * KIB
@@ -85,8 +84,7 @@ def tile_attend_cachewrite_kernel(tc, emb_words, emb_scales, wv, old, retain, of
         }
         for b in (2, 3):
             values[b] = keep.tile([P, I], F32, name="values%d" % b)
-        windows = [keep.tile([P, T], F32, name="window%d" % w) for w in range(WINDOWS - 1)]
-        windows.append(placed(AT_WINDOW2, [P, T], F32, "window2"))
+        windows = [keep.tile([P, T], F32, name="window%d" % w) for w in range(WINDOWS)]
 
         old_sb = [keep.tile([P, T], F32, name="old_sb%d" % b) for b in range(BLOCKS)]
         retain_rows = keep.tile([P, P], F32, name="retain_rows")
@@ -102,9 +100,8 @@ def tile_attend_cachewrite_kernel(tc, emb_words, emb_scales, wv, old, retain, of
         nc.vector.memset(pool_scales[:].bitcast(I32), 0)
         make_identity(nc, ident[:])
         nc.gpsimd.memset(retain_rows[:], 0.0)
-        for window in windows[0:2]:
-            nc.vector.memset(window[:, 0 : T // 2 + 1], 0.0)
-            nc.vector.memset(window[:, T // 2 + 1 :], 0.0)
+        for window in windows:
+            nc.vector.memset(window[:], 0.0)
 
         def load_wv(b, queue=nc.sync):
             queue.dma_start(out=wv_raw[b][:], in_=wv[:, b * P : (b + 1) * P].rearrange("(p j) e -> p j e", j=PACK))
@@ -185,7 +182,6 @@ def tile_attend_cachewrite_kernel(tc, emb_words, emb_scales, wv, old, retain, of
         half_lists = [emb_list[:, 0 : HALF // GROUP], emb_list[:, HALF // GROUP :]]
         nc.vector.tensor_copy(listed_scales[0][:], pool_scales[:].indirect(half_lists[0]))
         nc.vector.quantize_mx(out=codes0[:].bitcast(FP8X4), scales=wv_scales[:, 0:P], in_=wv_bf0[:])
-        nc.gpsimd.memset(windows[2][:], 0.0)
         for half in range(2):
             nc.vector.tensor_copy(listed_words[half][:], pool_words[:].indirect(half_lists[half]))
         nc.vector.tensor_copy(listed_scales[1][:], pool_scales[:].indirect(half_lists[1]))

@@ -31,12 +31,14 @@ WINDOWS = 3
 ALIGN = 64
 KIB = 1024
 
-AT_BF0 = 5 * KIB
-AT_BF1 = AT_BF0 + ALIGN - KIB
-AT_KEPT0 = AT_BF1 + ALIGN - 4 * KIB
+AT_KEPT0 = 0
+AT_BF1 = 4 * KIB - ALIGN
+AT_SCALES1 = AT_BF1 + KIB
+AT_QUADS = AT_SCALES1 - ALIGN
+AT_BF0 = 6 * KIB
+AT_WINDOW2 = 6 * KIB
 AT_RAW0 = 19 * KIB
 AT_RAW3 = 12 * KIB
-AT_WORDS = 22 * KIB
 AT_RAW1 = 14 * KIB
 AT_BF23 = 15 * KIB
 AT_CODES0 = 16 * KIB
@@ -56,10 +58,10 @@ def tile_attend_cachewrite_kernel(tc, emb_words, emb_scales, wv, old, retain, of
 
         emb_list = keep.tile([P, I // GROUP], U16, name="emb_list")
         place_list = keep.tile([P, I // GROUP], U16, name="place_list")
-        pool_words = placed(AT_WORDS, [P, U], U16, "pool_words")
+        pool_words = keep.tile([P, U], U16, name="pool_words", align_bytes=ALIGN)
         pool_scales = keep.tile([P, U], U8, name="pool_scales", align_bytes=ALIGN)
         listed_words = [keep.tile([P, HALF], U16, name="listed_words0", align_bytes=ALIGN), keep.tile([P, HALF], U16, name="listed_words1", align_bytes=ALIGN)]
-        listed_scales = [keep.tile([P, HALF], U8, name="listed_scales0", align_bytes=ALIGN), placed(AT_WORDS, [P, HALF], U8, "listed_scales1")]
+        listed_scales = [keep.tile([P, HALF], U8, name="listed_scales0", align_bytes=ALIGN), placed(AT_SCALES1, [P, HALF], U8, "listed_scales1")]
 
         wv_raw = [
             placed(AT_RAW0, [P, PACK, P], F32, "wv_raw0"),
@@ -84,12 +86,13 @@ def tile_attend_cachewrite_kernel(tc, emb_words, emb_scales, wv, old, retain, of
         }
         for b in (2, 3):
             values[b] = keep.tile([P, I], F32, name="values%d" % b)
-        windows = [keep.tile([P, T], F32, name="window%d" % w) for w in range(WINDOWS)]
+        windows = [keep.tile([P, T], F32, name="window%d" % w) for w in range(WINDOWS - 1)]
+        windows.append(placed(AT_WINDOW2, [P, T], F32, "window2"))
 
         old_sb = [keep.tile([P, T], F32, name="old_sb%d" % b) for b in range(BLOCKS)]
         retain_rows = keep.tile([P, P], F32, name="retain_rows")
         retain_cols = keep.tile([P, CHUNKS], F32, name="retain_cols")
-        retain_quads = placed(AT_BF1 + 2 * ALIGN, [P, 2, 2 * LINE], F32, "retain_quads")
+        retain_quads = placed(AT_QUADS, [P, 2, 4 * LINE], F32, "retain_quads")
         retain_half = [placed(AT_RAW0 - KIB, [P, BANK], F32, "retain_lo"), placed(AT_RAW0 + KIB, [P, BANK], F32, "retain_hi")]
         turned = [keep.tile([P, CHUNKS, P], F32, name="turned%d" % s) for s in range(2)]
         kept = [placed(AT_KEPT0, [P, T], F32, "kept0"), keep.tile([P, T], F32, name="kept1"), keep.tile([P, T], F32, name="kept2")]
@@ -100,7 +103,7 @@ def tile_attend_cachewrite_kernel(tc, emb_words, emb_scales, wv, old, retain, of
         nc.vector.memset(pool_scales[:].bitcast(I32), 0)
         make_identity(nc, ident[:])
         nc.gpsimd.memset(retain_rows[:], 0.0)
-        for window in windows:
+        for window in windows[0:2]:
             nc.vector.memset(window[:], 0.0)
 
         def load_wv(b, queue=nc.sync):
@@ -182,6 +185,7 @@ def tile_attend_cachewrite_kernel(tc, emb_words, emb_scales, wv, old, retain, of
         half_lists = [emb_list[:, 0 : HALF // GROUP], emb_list[:, HALF // GROUP :]]
         nc.vector.tensor_copy(listed_scales[0][:], pool_scales[:].indirect(half_lists[0]))
         nc.vector.quantize_mx(out=codes0[:].bitcast(FP8X4), scales=wv_scales[:, 0:P], in_=wv_bf0[:])
+        nc.gpsimd.memset(windows[2][:], 0.0)
         for half in range(2):
             nc.vector.tensor_copy(listed_words[half][:], pool_words[:].indirect(half_lists[half]))
         nc.vector.tensor_copy(listed_scales[1][:], pool_scales[:].indirect(half_lists[1]))
@@ -193,7 +197,19 @@ def tile_attend_cachewrite_kernel(tc, emb_words, emb_scales, wv, old, retain, of
             nc.scalar.copy(out=values[b, half][:], in_=bank[:, 0:HALF])
             scatter(b, half * HALF, (half + 1) * HALF, values[b, half][:])
 
-        half_step(0, 0, banks[0])
+        for n, bank in enumerate(banks[0:2]):
+            cols = slice(n * P, (n + 1) * P)
+            nc.tensor.matmul_mx(
+                out=bank[:, 0:P],
+                lhsT=wv_codes[0].bitcast(FP8X4),
+                lhsT_scale=wv_scales[:, 0:P],
+                rhs=listed_words[0][:, cols].bitcast(FP4X4),
+                rhs_scale=listed_scales[0][:, cols],
+                start=True,
+                stop=True,
+            )
+            nc.scalar.copy(out=values[0, 0][:, cols], in_=bank[:, 0:P])
+        scatter(0, 0, HALF, values[0, 0][:])
         half_step(1, 0, banks[1])
         half_step(0, 1, banks[1])
         multiply(0)
@@ -202,10 +218,12 @@ def tile_attend_cachewrite_kernel(tc, emb_words, emb_scales, wv, old, retain, of
         cast(3)
         nc.vector.quantize_mx(out=codes123[:, P:].bitcast(FP8X4), scales=wv_scales[:, 2 * P :], in_=wv_bf23[:])
         half_step(1, 1, banks[0])
-        for b in (2, 3):
-            for half in range(2):
-                project(b, half, banks[b][:, half * HALF : (half + 1) * HALF])
-            nc.scalar.copy(out=values[b][:], in_=banks[b][:])
+        for half in range(2):
+            project(2, half, banks[2 + half][:, 0:HALF])
+            nc.scalar.copy(out=values[2][:, half * HALF : (half + 1) * HALF], in_=banks[2 + half][:, 0:HALF])
+        for half in range(2):
+            project(3, half, banks[4][:, half * HALF : (half + 1) * HALF])
+        nc.scalar.copy(out=values[3][:], in_=banks[4][:])
         add_and_store(0, 1)
         add_and_store(1, 1)
 

@@ -30,6 +30,8 @@ GROUP = 16
 WINDOWS = 3
 ALIGN = 64
 KIB = 1024
+EARLY = 640
+POOL_END = 192
 
 AT_KEPT0 = 0
 AT_BF1 = 4 * KIB - ALIGN
@@ -37,7 +39,7 @@ AT_SCALES1 = AT_BF1 + KIB
 AT_QUADS = AT_SCALES1 - ALIGN
 AT_BF0 = 6 * KIB
 AT_WINDOW2 = 6 * KIB
-AT_RAW0 = 19 * KIB
+AT_RAW0 = 20 * KIB
 AT_RAW3 = 12 * KIB
 AT_RAW1 = 14 * KIB
 AT_BF23 = 15 * KIB
@@ -89,15 +91,17 @@ def tile_attend_cachewrite_kernel(tc, emb_words, emb_scales, wv, old, retain, of
         windows = [keep.tile([P, T], F32, name="window%d" % w) for w in range(WINDOWS - 1)]
         windows.append(placed(AT_WINDOW2, [P, T], F32, "window2"))
 
-        old_sb = [keep.tile([P, T], F32, name="old_sb%d" % b) for b in range(BLOCKS)]
+        old0 = [keep.tile([P, BANK], F32, name="old0_%d" % h) for h in range(T // BANK)]
+        old_sb = {b: keep.tile([P, T], F32, name="old_sb%d" % b) for b in range(1, BLOCKS)}
         retain_rows = keep.tile([P, P], F32, name="retain_rows")
         retain_cols = keep.tile([P, CHUNKS], F32, name="retain_cols")
         retain_quads = placed(AT_QUADS, [P, 2, 4 * LINE], F32, "retain_quads")
-        retain_half = [placed(AT_RAW0 - KIB, [P, BANK], F32, "retain_lo"), placed(AT_RAW0 + KIB, [P, BANK], F32, "retain_hi")]
+        retain_all = placed(AT_RAW0 - KIB, [P, T], F32, "retain_all")
         turned = [keep.tile([P, CHUNKS, P], F32, name="turned%d" % s) for s in range(2)]
         kept = [placed(AT_KEPT0, [P, T], F32, "kept0"), keep.tile([P, T], F32, name="kept1"), keep.tile([P, T], F32, name="kept2")]
-        kept_end = keep.tile([P, QUARTER], F32, name="kept_end")
-        result = [keep.tile([P, T], F32, name="result%d" % b) for b in range(BLOCKS)]
+        kept_end = keep.tile([P, POOL_END], F32, name="kept_end")
+        result = [placed(AT_BF23, [P, T], F32, "result0")]
+        result += [keep.tile([P, T], F32, name="result%d" % b) for b in range(1, BLOCKS)]
         ident = keep.tile([P, P], F32, name="ident")
 
         nc.vector.memset(pool_scales[:].bitcast(I32), 0)
@@ -121,7 +125,8 @@ def tile_attend_cachewrite_kernel(tc, emb_words, emb_scales, wv, old, retain, of
         nc.sync.dma_start(out=pool_words[:].bitcast(I32), in_=emb_words[0].bitcast(I32))
         load_wv(1)
         nc.sync.dma_start(place_list[:], offs2)
-        load_old(0)
+        for h in range(T // BANK):
+            nc.sync.dma_start(out=old0[h][:], in_=old[0:P, h * BANK : (h + 1) * BANK])
         load_old(1)
         load_wv(2)
         load_wv(3)
@@ -153,12 +158,12 @@ def tile_attend_cachewrite_kernel(tc, emb_words, emb_scales, wv, old, retain, of
         def spread_retain(h, bank):
             for c in range(LINE):
                 nc.tensor.transpose(bank[:, c * P : (c + 1) * P], retain_quads[:, h, c : c + 1].to_broadcast([P, P]), ident[:])
-            nc.scalar.copy(out=retain_half[h][:].rearrange("p (n c) -> p n c", c=LINE), in_=bank[:].rearrange("p (c n) -> p n c", c=LINE))
+            nc.scalar.copy(out=retain_all[:, h * BANK : (h + 1) * BANK].rearrange("p (n c) -> p n c", c=LINE), in_=bank[:].rearrange("p (c n) -> p n c", c=LINE))
 
-        def multiply(b):
-            for h in range(T // BANK):
-                cols = slice(h * BANK, (h + 1) * BANK)
-                nc.gpsimd.tensor_tensor(kept[b][:, cols], old_sb[b][:, cols], retain_half[h][:], MULT)
+        def multiply(b, lo, hi):
+            cols = slice(lo, hi)
+            src = old0[lo // BANK][:] if b == 0 else old_sb[b][:, cols]
+            nc.gpsimd.tensor_tensor(kept[b][:, cols], src, retain_all[:, cols], MULT)
 
         def add_and_store(b, pieces):
             for n in range(pieces):
@@ -212,8 +217,9 @@ def tile_attend_cachewrite_kernel(tc, emb_words, emb_scales, wv, old, retain, of
         scatter(0, 0, HALF, values[0, 0][:])
         half_step(1, 0, banks[1])
         half_step(0, 1, banks[1])
-        multiply(0)
-        multiply(1)
+        multiply(0, 0, BANK)
+        multiply(0, BANK, T)
+        multiply(1, 0, EARLY)
         cast(2)
         cast(3)
         nc.vector.quantize_mx(out=codes123[:, P:].bitcast(FP8X4), scales=wv_scales[:, 2 * P :], in_=wv_bf23[:])
@@ -225,6 +231,7 @@ def tile_attend_cachewrite_kernel(tc, emb_words, emb_scales, wv, old, retain, of
             project(3, half, banks[4][:, half * HALF : (half + 1) * HALF])
         nc.scalar.copy(out=values[3][:], in_=banks[4][:])
         add_and_store(0, 1)
+        multiply(1, EARLY, T)
         add_and_store(1, 1)
 
         nc.tensor.transpose(banks[1][:, 0:P], retain_rows[:], ident[:])
@@ -233,18 +240,19 @@ def tile_attend_cachewrite_kernel(tc, emb_words, emb_scales, wv, old, retain, of
         for h in range(T // BANK):
             nc.scalar.copy(out=kept[2][:, h * BANK : (h + 1) * BANK], in_=banks[4 + h][:])
         multiply_turned(3, [banks[2], banks[3]], banks[6:8])
-        nc.scalar.copy(out=kept_end[:], in_=banks[7][:, BANK - QUARTER :])
+        nc.scalar.copy(out=kept_end[:], in_=banks[7][:, BANK - POOL_END :])
 
         scatter(2, 0, I, values[2][:])
         add_and_store(2, 2)
         last = BLOCKS - 1
         scatter(last, 0, I, values[last][:])
         window = windows[last % WINDOWS]
+        edges = [0, QUARTER, BANK, T - POOL_END, T]
         for n in range(4):
-            cols = slice(n * QUARTER, (n + 1) * QUARTER)
+            cols = slice(edges[n], edges[n + 1])
             if n < 3:
-                h, c = divmod(n * QUARTER, BANK)
-                nc.vector.tensor_tensor(result[last][:, cols], banks[6 + h][:, c : c + QUARTER], window[:, cols], ADD)
+                h, c = divmod(edges[n], BANK)
+                nc.vector.tensor_tensor(result[last][:, cols], banks[6 + h][:, c : c + edges[n + 1] - edges[n]], window[:, cols], ADD)
             else:
                 nc.gpsimd.tensor_tensor(result[last][:, cols], kept_end[:], window[:, cols], ADD)
             queue = nc.sync if n % 2 == 0 else nc.scalar

@@ -38,7 +38,6 @@ AT_BF1 = 4 * KIB - ALIGN
 AT_SCALES1 = AT_BF1 + KIB
 AT_QUADS = AT_SCALES1 - ALIGN
 AT_BF0 = 6 * KIB
-AT_WINDOW2 = 6 * KIB
 AT_RAW0 = 20 * KIB
 AT_RAW3 = 12 * KIB
 AT_RAW1 = 14 * KIB
@@ -81,15 +80,14 @@ def tile_attend_cachewrite_kernel(tc, emb_words, emb_scales, wv, old, retain, of
         wv_scales = keep.tile([P, E], U8, name="wv_scales", align_bytes=ALIGN)
 
         values = {
-            (0, 0): placed(AT_RAW1, [P, HALF], F32, "values0a"),
+            (0, 0): keep.tile([P, HALF], F32, name="values0a"),
             (1, 0): keep.tile([P, HALF], F32, name="values1a"),
             (0, 1): keep.tile([P, HALF], F32, name="values0b"),
             (1, 1): placed(AT_RAW3, [P, HALF], F32, "values1b"),
         }
         for b in (2, 3):
             values[b] = keep.tile([P, I], F32, name="values%d" % b)
-        windows = [keep.tile([P, T], F32, name="window%d" % w) for w in range(WINDOWS - 1)]
-        windows.append(placed(AT_WINDOW2, [P, T], F32, "window2"))
+        windows = [keep.tile([P, T], F32, name="window%d" % w) for w in range(WINDOWS)]
 
         old0 = [keep.tile([P, BANK], F32, name="old0_%d" % h) for h in range(T // BANK)]
         old_sb = {b: keep.tile([P, T], F32, name="old_sb%d" % b) for b in range(1, BLOCKS)}
@@ -107,7 +105,7 @@ def tile_attend_cachewrite_kernel(tc, emb_words, emb_scales, wv, old, retain, of
         nc.vector.memset(pool_scales[:].bitcast(I32), 0)
         make_identity(nc, ident[:])
         nc.gpsimd.memset(retain_rows[:], 0.0)
-        for window in windows[0:2]:
+        for window in windows:
             nc.vector.memset(window[:], 0.0)
 
         def load_wv(b, queue=nc.sync):
@@ -190,11 +188,17 @@ def tile_attend_cachewrite_kernel(tc, emb_words, emb_scales, wv, old, retain, of
         half_lists = [emb_list[:, 0 : HALF // GROUP], emb_list[:, HALF // GROUP :]]
         nc.vector.tensor_copy(listed_scales[0][:], pool_scales[:].indirect(half_lists[0]))
         nc.vector.quantize_mx(out=codes0[:].bitcast(FP8X4), scales=wv_scales[:, 0:P], in_=wv_bf0[:])
-        nc.gpsimd.memset(windows[2][:], 0.0)
         for half in range(2):
             nc.vector.tensor_copy(listed_words[half][:], pool_words[:].indirect(half_lists[half]))
         nc.vector.tensor_copy(listed_scales[1][:], pool_scales[:].indirect(half_lists[1]))
-        cast(1)
+        nc.gpsimd.tensor_scalar(
+            out=wv_bf1[:].rearrange("p (c j) -> p c j", j=PACK),
+            in0=wv_raw[1][:].rearrange("p j c -> p c j"),
+            scalar1=1.0,
+            scalar2=0.0,
+            op0=MULT,
+            op1=ADD,
+        )
         nc.vector.quantize_mx(out=wv_codes[1].bitcast(FP8X4), scales=wv_scales[:, P : 2 * P], in_=wv_bf1[:])
 
         def half_step(b, half, bank):

@@ -30,7 +30,8 @@ GROUP = 16
 WINDOWS = 3
 ALIGN = 64
 KIB = 1024
-EARLY = 640
+EARLY = 576
+FIRST1 = 224
 POOL_END = 192
 
 AT_KEPT0 = 0
@@ -39,7 +40,6 @@ AT_SCALES1 = AT_BF1 + KIB
 AT_QUADS = AT_SCALES1 - ALIGN
 AT_BF0 = 6 * KIB
 AT_RAW0 = 20 * KIB
-AT_RAW3 = 12 * KIB
 AT_RAW1 = 14 * KIB
 AT_BF23 = 15 * KIB
 AT_CODES0 = 16 * KIB
@@ -68,7 +68,7 @@ def tile_attend_cachewrite_kernel(tc, emb_words, emb_scales, wv, old, retain, of
             placed(AT_RAW0, [P, PACK, P], F32, "wv_raw0"),
             placed(AT_RAW1, [P, PACK, P], F32, "wv_raw1"),
             keep.tile([P, PACK, P], F32, name="wv_raw2"),
-            placed(AT_RAW3, [P, PACK, P], F32, "wv_raw3"),
+            keep.tile([P, PACK, P], F32, name="wv_raw3"),
         ]
         wv_bf0 = placed(AT_BF0, [P, P * PACK], BF16, "wv_bf0")
         wv_bf1 = placed(AT_BF1, [P, P * PACK], BF16, "wv_bf1")
@@ -81,11 +81,9 @@ def tile_attend_cachewrite_kernel(tc, emb_words, emb_scales, wv, old, retain, of
 
         values = {
             (0, 0): keep.tile([P, HALF], F32, name="values0a"),
-            (1, 0): keep.tile([P, HALF], F32, name="values1a"),
             (0, 1): keep.tile([P, HALF], F32, name="values0b"),
-            (1, 1): placed(AT_RAW3, [P, HALF], F32, "values1b"),
         }
-        for b in (2, 3):
+        for b in (1, 2, 3):
             values[b] = keep.tile([P, I], F32, name="values%d" % b)
         windows = [keep.tile([P, T], F32, name="window%d" % w) for w in range(WINDOWS)]
 
@@ -219,7 +217,9 @@ def tile_attend_cachewrite_kernel(tc, emb_words, emb_scales, wv, old, retain, of
             )
             nc.scalar.copy(out=values[0, 0][:, cols], in_=bank[:, 0:P])
         scatter(0, 0, HALF, values[0, 0][:])
-        half_step(1, 0, banks[1])
+        project(1, 0, banks[1][:, 0:HALF])
+        nc.scalar.copy(out=values[1][:, 0:HALF], in_=banks[1][:, 0:HALF])
+        scatter(1, 0, FIRST1, values[1][:, 0:FIRST1])
         half_step(0, 1, banks[1])
         multiply(0, 0, BANK)
         multiply(0, BANK, T)
@@ -227,7 +227,9 @@ def tile_attend_cachewrite_kernel(tc, emb_words, emb_scales, wv, old, retain, of
         cast(2)
         cast(3)
         nc.vector.quantize_mx(out=codes123[:, P:].bitcast(FP8X4), scales=wv_scales[:, 2 * P :], in_=wv_bf23[:])
-        half_step(1, 1, banks[0])
+        project(1, 1, banks[1][:, 0:HALF])
+        nc.scalar.copy(out=values[1][:, HALF:], in_=banks[1][:, 0:HALF])
+        scatter(1, FIRST1, I, values[1][:, FIRST1:])
         for half in range(2):
             project(2, half, banks[2 + half][:, 0:HALF])
             nc.scalar.copy(out=values[2][:, half * HALF : (half + 1) * HALF], in_=banks[2 + half][:, 0:HALF])
@@ -240,7 +242,7 @@ def tile_attend_cachewrite_kernel(tc, emb_words, emb_scales, wv, old, retain, of
 
         nc.tensor.transpose(banks[1][:, 0:P], retain_rows[:], ident[:])
         nc.scalar.copy(out=retain_cols[:], in_=banks[1][:, 0:CHUNKS])
-        multiply_turned(2, [banks[1], banks[0]], banks[4:6])
+        multiply_turned(2, banks[0:2], banks[4:6])
         for h in range(T // BANK):
             nc.scalar.copy(out=kept[2][:, h * BANK : (h + 1) * BANK], in_=banks[4 + h][:])
         multiply_turned(3, [banks[2], banks[3]], banks[6:8])

@@ -101,8 +101,9 @@ def tile_attend_cachewrite_kernel(tc, emb_words, emb_scales, wv, old, retain, of
         ident = keep.tile([P, P], F32, name="ident")
 
         nc.vector.memset(pool_scales[:].bitcast(I32), 0)
-        make_identity(nc, ident[:])
-        nc.gpsimd.memset(retain_rows[:], 0.0)
+        nc.vector.memset(ident[:], 0.0)
+        make_identity(nc, ident[:], nomemset=True)
+        nc.vector.memset(retain_rows[:], 0.0)
         for window in windows:
             nc.vector.memset(window[:], 0.0)
 

@@ -107,14 +107,14 @@ def tile_attend_cachewrite_kernel(tc, emb_words, emb_scales, wv, old, retain, of
         for window in windows:
             nc.vector.memset(window[:], 0.0)
 
-        def load_wv(b, queue=nc.sync):
-            queue.dma_start(out=wv_raw[b][:], in_=wv[:, b * P : (b + 1) * P].rearrange("(p j) e -> p j e", j=PACK))
+        def load_wv(b):
+            nc.sync.dma_start(out=wv_raw[b][:], in_=wv[:, b * P : (b + 1) * P].rearrange("(p j) e -> p j e", j=PACK))
 
         def load_old(b):
             nc.sync.dma_start(out=old_sb[b][:], in_=old[b * P : (b + 1) * P, :])
 
         nc.sync.dma_start(out=retain_quads[:, :, 0:LINE], in_=retain.rearrange("o (h p c) -> (o p) h c", h=2, c=LINE))
-        load_wv(0, nc.scalar)
+        load_wv(0)
         nc.sync.dma_start(emb_list[:], offs)
         scale_rows = emb_scales[0].rearrange("(q r) u -> r q u", r=4)
         for r in range(4):

@@ -21,6 +21,7 @@ MULT = mybir.AluOpType.mult
 P = 128
 PACK = 4
 LINE = 4
+OCT = 8
 BLOCKS = E // P
 CHUNKS = T // P
 BANK = 512
@@ -91,7 +92,7 @@ def tile_attend_cachewrite_kernel(tc, emb_words, emb_scales, wv, old, retain, of
         old_sb = {b: keep.tile([P, T], F32, name="old_sb%d" % b) for b in range(1, BLOCKS)}
         retain_rows = keep.tile([P, P], F32, name="retain_rows")
         retain_cols = keep.tile([P, CHUNKS], F32, name="retain_cols")
-        retain_quads = placed(AT_QUADS, [P, 2, 4 * LINE], F32, "retain_quads")
+        retain_octs = placed(AT_QUADS, [P, 4 * OCT], F32, "retain_octs")
         retain_all = placed(AT_RAW0 - KIB, [P, T], F32, "retain_all")
         turned = [keep.tile([P, CHUNKS, P], F32, name="turned%d" % s) for s in range(2)]
         kept = [placed(AT_KEPT0, [P, T], F32, "kept0"), keep.tile([P, T], F32, name="kept1"), keep.tile([P, T], F32, name="kept2")]
@@ -113,7 +114,7 @@ def tile_attend_cachewrite_kernel(tc, emb_words, emb_scales, wv, old, retain, of
         def load_old(b):
             nc.sync.dma_start(out=old_sb[b][:], in_=old[b * P : (b + 1) * P, :])
 
-        nc.sync.dma_start(out=retain_quads[:, :, 0:LINE], in_=retain.rearrange("o (h p c) -> (o p) h c", h=2, c=LINE))
+        nc.sync.dma_start(out=retain_octs[:, 0:OCT], in_=retain.rearrange("o (p c) -> (o p) c", c=OCT))
         load_wv(0)
         nc.sync.dma_start(emb_list[:], offs)
         scale_rows = emb_scales[0].rearrange("(q r) u -> r q u", r=4)
@@ -154,8 +155,8 @@ def tile_attend_cachewrite_kernel(tc, emb_words, emb_scales, wv, old, retain, of
 
         def spread_retain(h, bank):
             for c in range(LINE):
-                nc.tensor.transpose(bank[:, c * P : (c + 1) * P], retain_quads[:, h, c : c + 1].to_broadcast([P, P]), ident[:])
-            nc.scalar.copy(out=retain_all[:, h * BANK : (h + 1) * BANK].rearrange("p (n c) -> p n c", c=LINE), in_=bank[:].rearrange("p (c n) -> p n c", c=LINE))
+                nc.tensor.transpose(bank[:, c * P : (c + 1) * P], retain_octs[:, h * LINE + c : h * LINE + c + 1].to_broadcast([P, P]), ident[:])
+            nc.scalar.copy(out=retain_all[:].rearrange("p (n c) -> p n c", c=OCT)[:, :, h * LINE : (h + 1) * LINE], in_=bank[:].rearrange("p (c n) -> p n c", c=LINE))
 
         def multiply(b, lo, hi):
             cols = slice(lo, hi)

@@ -263,5 +263,4 @@ def tile_attend_cachewrite_kernel(tc, emb_words, emb_scales, wv, old, retain, of
                 nc.vector.tensor_tensor(result[last][:, cols], banks[6 + h][:, c : c + edges[n + 1] - edges[n]], window[:, cols], ADD)
             else:
                 nc.gpsimd.tensor_tensor(result[last][:, cols], kept_end[:], window[:, cols], ADD)
-            queue = nc.sync if n % 2 == 0 else nc.scalar
-            queue.dma_start(out=out[last * P :, cols], in_=result[last][:, cols])
+            nc.sync.dma_start(out=out[last * P :, cols], in_=result[last][:, cols])

@@ -31,7 +31,6 @@ GROUP = 16
 WINDOWS = 3
 ALIGN = 64
 KIB = 1024
-EARLY = 576
 FIRST1 = 224
 POOL_END = 192
 
@@ -68,9 +67,9 @@ def tile_attend_cachewrite_kernel(tc, emb_words, emb_scales, wv, old, retain, of
         wv_raw = [
             placed(AT_RAW0, [P, PACK, P], F32, "wv_raw0"),
             placed(AT_RAW1, [P, PACK, P], F32, "wv_raw1"),
-            keep.tile([P, PACK, P], F32, name="wv_raw2"),
-            keep.tile([P, PACK, P], F32, name="wv_raw3"),
         ]
+        wv_raw23 = keep.tile([P, PACK, 2 * P], F32, name="wv_raw23")
+        wv_src = [wv_raw[0][:], wv_raw[1][:], wv_raw23[:, :, 0:P], wv_raw23[:, :, P:]]
         wv_bf0 = placed(AT_BF0, [P, P * PACK], BF16, "wv_bf0")
         wv_bf1 = placed(AT_BF1, [P, P * PACK], BF16, "wv_bf1")
         wv_bf23 = placed(AT_BF23, [P, 2 * P * PACK], BF16, "wv_bf23")
@@ -88,8 +87,8 @@ def tile_attend_cachewrite_kernel(tc, emb_words, emb_scales, wv, old, retain, of
             values[b] = keep.tile([P, I], F32, name="values%d" % b)
         windows = [keep.tile([P, T], F32, name="window%d" % w) for w in range(WINDOWS)]
 
-        old0 = [keep.tile([P, BANK], F32, name="old0_%d" % h) for h in range(T // BANK)]
-        old_sb = {b: keep.tile([P, T], F32, name="old_sb%d" % b) for b in range(1, BLOCKS)}
+        old_half = {(b, h): keep.tile([P, BANK], F32, name="old%d_%d" % (b, h)) for b in range(2) for h in range(T // BANK)}
+        old_sb = {b: keep.tile([P, T], F32, name="old_sb%d" % b) for b in range(2, BLOCKS)}
         retain_rows = keep.tile([P, P], F32, name="retain_rows")
         retain_cols = keep.tile([P, CHUNKS], F32, name="retain_cols")
         retain_octs = placed(AT_QUADS, [P, 4 * OCT], F32, "retain_octs")
@@ -111,6 +110,9 @@ def tile_attend_cachewrite_kernel(tc, emb_words, emb_scales, wv, old, retain, of
         def load_wv(b):
             nc.sync.dma_start(out=wv_raw[b][:], in_=wv[:, b * P : (b + 1) * P].rearrange("(p j) e -> p j e", j=PACK))
 
+        def load_old_half(b, h):
+            nc.sync.dma_start(out=old_half[b, h][:], in_=old[b * P : (b + 1) * P, h * BANK : (h + 1) * BANK])
+
         def load_old(b):
             nc.sync.dma_start(out=old_sb[b][:], in_=old[b * P : (b + 1) * P, :])
 
@@ -123,11 +125,11 @@ def tile_attend_cachewrite_kernel(tc, emb_words, emb_scales, wv, old, retain, of
         nc.sync.dma_start(out=pool_words[:].bitcast(I32), in_=emb_words[0].bitcast(I32))
         load_wv(1)
         nc.sync.dma_start(place_list[:], offs2)
-        for h in range(T // BANK):
-            nc.sync.dma_start(out=old0[h][:], in_=old[0:P, h * BANK : (h + 1) * BANK])
-        load_old(1)
-        load_wv(2)
-        load_wv(3)
+        load_old_half(0, 0)
+        load_old_half(0, 1)
+        load_old_half(1, 0)
+        nc.sync.dma_start(out=wv_raw23[:], in_=wv[:, 2 * P :].rearrange("(p j) e -> p j e", j=PACK))
+        load_old_half(1, 1)
         nc.sync.dma_start(out=retain_rows[0:CHUNKS, :], in_=retain.rearrange("o (c p) -> (o c) p", p=P))
         for b in range(2, BLOCKS):
             load_old(b)
@@ -135,7 +137,7 @@ def tile_attend_cachewrite_kernel(tc, emb_words, emb_scales, wv, old, retain, of
         def cast(b):
             nc.scalar.activation(
                 out=wv_bf[b].rearrange("p (c i j) -> p c j i", i=LINE, j=PACK),
-                in_=wv_raw[b][:].rearrange("p j (c i) -> p c j i", i=LINE),
+                in_=wv_src[b].rearrange("p j (c i) -> p c j i", i=LINE),
                 func=COPY,
             )
 
@@ -158,10 +160,9 @@ def tile_attend_cachewrite_kernel(tc, emb_words, emb_scales, wv, old, retain, of
                 nc.tensor.transpose(bank[:, c * P : (c + 1) * P], retain_octs[:, h * LINE + c : h * LINE + c + 1].to_broadcast([P, P]), ident[:])
             nc.scalar.copy(out=retain_all[:].rearrange("p (n c) -> p n c", c=OCT)[:, :, h * LINE : (h + 1) * LINE], in_=bank[:].rearrange("p (c n) -> p n c", c=LINE))
 
-        def multiply(b, lo, hi):
-            cols = slice(lo, hi)
-            src = old0[lo // BANK][:] if b == 0 else old_sb[b][:, cols]
-            nc.gpsimd.tensor_tensor(kept[b][:, cols], src, retain_all[:, cols], MULT)
+        def multiply(b, h):
+            cols = slice(h * BANK, (h + 1) * BANK)
+            nc.gpsimd.tensor_tensor(kept[b][:, cols], old_half[b, h][:], retain_all[:, cols], MULT)
 
         def add_and_store(b, pieces):
             for n in range(pieces):
@@ -223,9 +224,9 @@ def tile_attend_cachewrite_kernel(tc, emb_words, emb_scales, wv, old, retain, of
         nc.scalar.copy(out=values[1][:, 0:HALF], in_=banks[1][:, 0:HALF])
         scatter(1, 0, FIRST1, values[1][:, 0:FIRST1])
         half_step(0, 1, banks[1])
-        multiply(0, 0, BANK)
-        multiply(0, BANK, T)
-        multiply(1, 0, EARLY)
+        multiply(0, 0)
+        multiply(0, 1)
+        multiply(1, 0)
         cast(2)
         cast(3)
         nc.vector.quantize_mx(out=codes123[:, P:].bitcast(FP8X4), scales=wv_scales[:, 2 * P :], in_=wv_bf23[:])
@@ -239,7 +240,7 @@ def tile_attend_cachewrite_kernel(tc, emb_words, emb_scales, wv, old, retain, of
             project(3, half, banks[4][:, half * HALF : (half + 1) * HALF])
         nc.scalar.copy(out=values[3][:], in_=banks[4][:])
         add_and_store(0, 1)
-        multiply(1, EARLY, T)
+        multiply(1, 1)
         add_and_store(1, 1)
 
         nc.tensor.transpose(banks[1][:, 0:P], retain_rows[:], ident[:])

@@ -121,7 +121,8 @@ def tile_attend_cachewrite_kernel(tc, emb_words, emb_scales, wv, old, retain, of
         nc.sync.dma_start(emb_list[:], offs)
         scale_rows = emb_scales[0].rearrange("(q r) u -> r q u", r=4)
         for r in range(4):
-            nc.sync.dma_start(out=pool_scales[r:P:32, :].bitcast(I32), in_=scale_rows[r].bitcast(I32))
+            queue = nc.sync if r % 2 == 0 else nc.scalar
+            queue.dma_start(out=pool_scales[r:P:32, :].bitcast(I32), in_=scale_rows[r].bitcast(I32))
         nc.sync.dma_start(out=pool_words[:].bitcast(I32), in_=emb_words[0].bitcast(I32))
         load_wv(1)
         nc.sync.dma_start(place_list[:], offs2)
@@ -182,7 +183,11 @@ def tile_attend_cachewrite_kernel(tc, emb_words, emb_scales, wv, old, retain, of
                 h, c = divmod(chunk, BANK // P)
                 nc.tensor.transpose(back[h][:, c * P : (c + 1) * P], turned[b % 2][:, chunk], ident[:])
 
-        cast(0)
+        for engine_copy, cols in ((nc.vector.tensor_copy, slice(0, P // 2)), (nc.scalar.copy, slice(P // 2, P))):
+            engine_copy(
+                out=wv_bf[0][:, cols.start * PACK : cols.stop * PACK].rearrange("p (c i j) -> p c j i", i=LINE, j=PACK),
+                in_=wv_src[0][:, :, cols].rearrange("p j (c i) -> p c j i", i=LINE),
+            )
         spread_retain(0, banks[0])
         spread_retain(1, banks[1])
 

@@ -121,8 +121,7 @@ def tile_attend_cachewrite_kernel(tc, emb_words, emb_scales, wv, old, retain, of
         nc.sync.dma_start(emb_list[:], offs)
         scale_rows = emb_scales[0].rearrange("(q r) u -> r q u", r=4)
         for r in range(4):
-            queue = nc.sync if r % 2 == 0 else nc.scalar
-            queue.dma_start(out=pool_scales[r:P:32, :].bitcast(I32), in_=scale_rows[r].bitcast(I32))
+            nc.sync.dma_start(out=pool_scales[r:P:32, :].bitcast(I32), in_=scale_rows[r].bitcast(I32))
         nc.sync.dma_start(out=pool_words[:].bitcast(I32), in_=emb_words[0].bitcast(I32))
         load_wv(1)
         nc.sync.dma_start(place_list[:], offs2)

@@ -33,6 +33,7 @@ ALIGN = 64
 KIB = 1024
 FIRST1 = 224
 POOL_END = 192
+VECTOR_COLS = 96
 
 AT_KEPT0 = 0
 AT_BF1 = 4 * KIB - ALIGN
@@ -85,7 +86,8 @@ def tile_attend_cachewrite_kernel(tc, emb_words, emb_scales, wv, old, retain, of
         }
         for b in (1, 2, 3):
             values[b] = keep.tile([P, I], F32, name="values%d" % b)
-        windows = [keep.tile([P, T], F32, name="window%d" % w) for w in range(WINDOWS)]
+        windows = [keep.tile([P, T], F32, name="window%d" % w) for w in range(WINDOWS - 1)]
+        windows.append(placed(AT_BF0, [P, T], F32, "window2"))
 
         old_half = {(b, h): keep.tile([P, BANK], F32, name="old%d_%d" % (b, h)) for b in range(2) for h in range(T // BANK)}
         old_sb = {b: keep.tile([P, T], F32, name="old_sb%d" % b) for b in range(2, BLOCKS)}
@@ -104,7 +106,7 @@ def tile_attend_cachewrite_kernel(tc, emb_words, emb_scales, wv, old, retain, of
         nc.vector.memset(ident[:], 0.0)
         make_identity(nc, ident[:], nomemset=True)
         nc.vector.memset(retain_rows[:], 0.0)
-        for window in windows:
+        for window in windows[:-1]:
             nc.vector.memset(window[:], 0.0)
 
         def load_wv(b):
@@ -182,7 +184,7 @@ def tile_attend_cachewrite_kernel(tc, emb_words, emb_scales, wv, old, retain, of
                 h, c = divmod(chunk, BANK // P)
                 nc.tensor.transpose(back[h][:, c * P : (c + 1) * P], turned[b % 2][:, chunk], ident[:])
 
-        for engine_copy, cols in ((nc.vector.tensor_copy, slice(0, P // 2)), (nc.scalar.copy, slice(P // 2, P))):
+        for engine_copy, cols in ((nc.vector.tensor_copy, slice(0, VECTOR_COLS)), (nc.scalar.copy, slice(VECTOR_COLS, P))):
             engine_copy(
                 out=wv_bf[0][:, cols.start * PACK : cols.stop * PACK].rearrange("p (c i j) -> p c j i", i=LINE, j=PACK),
                 in_=wv_src[0][:, :, cols].rearrange("p j (c i) -> p c j i", i=LINE),
@@ -193,16 +195,21 @@ def tile_attend_cachewrite_kernel(tc, emb_words, emb_scales, wv, old, retain, of
         half_lists = [emb_list[:, 0 : HALF // GROUP], emb_list[:, HALF // GROUP :]]
         nc.vector.tensor_copy(listed_scales[0][:], pool_scales[:].indirect(half_lists[0]))
         nc.vector.quantize_mx(out=codes0[:].bitcast(FP8X4), scales=wv_scales[:, 0:P], in_=wv_bf0[:])
+        nc.gpsimd.memset(windows[-1][:], 0.0)
         for half in range(2):
             nc.vector.tensor_copy(listed_words[half][:], pool_words[:].indirect(half_lists[half]))
         nc.vector.tensor_copy(listed_scales[1][:], pool_scales[:].indirect(half_lists[1]))
         nc.gpsimd.tensor_scalar(
-            out=wv_bf1[:].rearrange("p (c j) -> p c j", j=PACK),
-            in0=wv_raw[1][:].rearrange("p j c -> p c j"),
+            out=wv_bf1[:, 0 : P // 2 * PACK].rearrange("p (c j) -> p c j", j=PACK),
+            in0=wv_raw[1][:, :, 0 : P // 2].rearrange("p j c -> p c j"),
             scalar1=1.0,
             scalar2=0.0,
             op0=MULT,
             op1=ADD,
+        )
+        nc.scalar.copy(
+            out=wv_bf1[:, P // 2 * PACK :].rearrange("p (c i j) -> p c j i", i=LINE, j=PACK),
+            in_=wv_raw[1][:, :, P // 2 :].rearrange("p j (c i) -> p c j i", i=LINE),
         )
         nc.vector.quantize_mx(out=wv_codes[1].bitcast(FP8X4), scales=wv_scales[:, P : 2 * P], in_=wv_bf1[:])
 

@@ -31,7 +31,7 @@ GROUP = 16
 WINDOWS = 3
 ALIGN = 64
 KIB = 1024
-FIRST1 = 224
+FIRST1 = 192
 POOL_END = 192
 VECTOR_COLS = 96
 

@@ -21,29 +21,30 @@ MULT = mybir.AluOpType.mult
 P = 128
 PACK = 4
 LINE = 4
-OCT = 8
-BLOCKS = E // P
-CHUNKS = T // P
 BANK = 512
 HALF = I // 2
-QUARTER = T // 4
 GROUP = 16
-WINDOWS = 3
 ALIGN = 64
 KIB = 1024
-FIRST1 = 192
-POOL_END = 192
 VECTOR_COLS = 96
+EARLY_COLS = 512
+VECTOR_SLOTS3 = 256
 
-AT_KEPT0 = 0
-AT_BF1 = 4 * KIB - ALIGN
-AT_SCALES1 = AT_BF1 + KIB
-AT_QUADS = AT_SCALES1 - ALIGN
-AT_BF0 = 6 * KIB
-AT_RAW0 = 20 * KIB
-AT_RAW1 = 14 * KIB
-AT_BF23 = 15 * KIB
-AT_CODES0 = 16 * KIB
+AT_BF1 = 0
+AT_WORDS0 = AT_BF1 + KIB
+AT_WORDS1 = AT_WORDS0 + 2 * HALF
+AT_QUADS = AT_WORDS0 - ALIGN
+QUADS_BYTES = AT_WORDS1 + ALIGN - AT_QUADS
+AT_BF0 = 4 * KIB
+AT_RAW0 = 8 * KIB
+AT_RAW23 = 12 * KIB
+AT_KEPT12 = 16 * KIB
+AT_BF23 = AT_KEPT12 + 8 * KIB - ALIGN
+AT_KEPT0B = AT_BF23 + 2 * KIB - ALIGN
+AT_LATE = AT_KEPT0B + 4 * (T - EARLY_COLS) - ALIGN
+AT_SCALES1 = AT_LATE + 8 * KIB
+AT_RAW1 = AT_BF23
+RAW1_BYTES = AT_SCALES1 + ALIGN - AT_RAW1
 
 
 def tile_attend_cachewrite_kernel(tc, emb_words, emb_scales, wv, old, retain, offs, offs2, out):
@@ -57,222 +58,189 @@ def tile_attend_cachewrite_kernel(tc, emb_words, emb_scales, wv, old, retain, of
             return shared.tile(shape, dtype, name=name, offset=offset, align_bytes=ALIGN)
 
         banks = [psum.tile([P, BANK], F32, name="bank%d" % n) for n in range(8)]
+        retain_banks = banks[0:2]
 
         emb_list = keep.tile([P, I // GROUP], U16, name="emb_list")
         place_list = keep.tile([P, I // GROUP], U16, name="place_list")
         pool_words = keep.tile([P, U], U16, name="pool_words", align_bytes=ALIGN)
         pool_scales = keep.tile([P, U], U8, name="pool_scales", align_bytes=ALIGN)
-        listed_words = [keep.tile([P, HALF], U16, name="listed_words0", align_bytes=ALIGN), keep.tile([P, HALF], U16, name="listed_words1", align_bytes=ALIGN)]
+        listed_words = [placed(AT_WORDS0, [P, HALF], U16, "listed_words0"), placed(AT_WORDS1, [P, HALF], U16, "listed_words1")]
         listed_scales = [keep.tile([P, HALF], U8, name="listed_scales0", align_bytes=ALIGN), placed(AT_SCALES1, [P, HALF], U8, "listed_scales1")]
 
-        wv_raw = [
-            placed(AT_RAW0, [P, PACK, P], F32, "wv_raw0"),
-            placed(AT_RAW1, [P, PACK, P], F32, "wv_raw1"),
-        ]
-        wv_raw23 = keep.tile([P, PACK, 2 * P], F32, name="wv_raw23")
-        wv_src = [wv_raw[0][:], wv_raw[1][:], wv_raw23[:, :, 0:P], wv_raw23[:, :, P:]]
+        wv_raw0 = placed(AT_RAW0, [P, PACK, P], F32, "wv_raw0")
+        wv_raw1 = placed(AT_RAW1, [P, RAW1_BYTES // 4], F32, "wv_raw1")[:, 0 : PACK * P].rearrange("p (j e) -> p j e", j=PACK)
+        wv_raw23 = placed(AT_RAW23, [P, PACK, 2 * P], F32, "wv_raw23")
         wv_bf0 = placed(AT_BF0, [P, P * PACK], BF16, "wv_bf0")
         wv_bf1 = placed(AT_BF1, [P, P * PACK], BF16, "wv_bf1")
         wv_bf23 = placed(AT_BF23, [P, 2 * P * PACK], BF16, "wv_bf23")
-        wv_bf = [wv_bf0[:], wv_bf1[:], wv_bf23[:, 0 : P * PACK], wv_bf23[:, P * PACK :]]
-        codes0 = placed(AT_CODES0, [P, P], U32, "codes0")
-        codes123 = keep.tile([P, E - P], U32, name="codes123", align_bytes=ALIGN)
-        wv_codes = [codes0[:]] + [codes123[:, n * P : (n + 1) * P] for n in range(BLOCKS - 1)]
+        wv_codes = keep.tile([P, E], U32, name="wv_codes", align_bytes=ALIGN)
         wv_scales = keep.tile([P, E], U8, name="wv_scales", align_bytes=ALIGN)
 
-        values = {
-            (0, 0): keep.tile([P, HALF], F32, name="values0a"),
-            (0, 1): keep.tile([P, HALF], F32, name="values0b"),
-        }
-        for b in (1, 2, 3):
-            values[b] = keep.tile([P, I], F32, name="values%d" % b)
-        windows = [keep.tile([P, T], F32, name="window%d" % w) for w in range(WINDOWS - 1)]
-        windows.append(placed(AT_BF0, [P, T], F32, "window2"))
+        first0 = keep.tile([P, HALF], F32, name="first0")
+        first1 = keep.tile([P, HALF], F32, name="first1")
+        second0 = keep.tile([P, HALF], F32, name="second0")
+        second1 = placed(AT_RAW23 + 4 * EARLY_COLS, [P, HALF], F32, "second1")
+        values2 = keep.tile([P, I], F32, name="values2")
+        values3 = keep.tile([P, I], F32, name="values3")
+        window0 = keep.tile([P, T], F32, name="window0")
+        window1 = keep.tile([P, T], F32, name="window1")
+        window2 = placed(AT_BF0, [P, T], F32, "window2")
 
-        old_half = {(b, h): keep.tile([P, BANK], F32, name="old%d_%d" % (b, h)) for b in range(2) for h in range(T // BANK)}
-        old_sb = {b: keep.tile([P, T], F32, name="old_sb%d" % b) for b in range(2, BLOCKS)}
-        retain_rows = keep.tile([P, P], F32, name="retain_rows")
-        retain_cols = keep.tile([P, CHUNKS], F32, name="retain_cols")
-        retain_octs = placed(AT_QUADS, [P, 4 * OCT], F32, "retain_octs")
-        retain_all = placed(AT_RAW0 - KIB, [P, T], F32, "retain_all")
-        turned = [keep.tile([P, CHUNKS, P], F32, name="turned%d" % s) for s in range(2)]
-        kept = [placed(AT_KEPT0, [P, T], F32, "kept0"), keep.tile([P, T], F32, name="kept1"), keep.tile([P, T], F32, name="kept2")]
-        kept_end = keep.tile([P, POOL_END], F32, name="kept_end")
-        result = [placed(AT_BF23, [P, T], F32, "result0")]
-        result += [keep.tile([P, T], F32, name="result%d" % b) for b in range(1, BLOCKS)]
+        old0 = [keep.tile([P, EARLY_COLS], F32, name="old0a"), keep.tile([P, T - EARLY_COLS], F32, name="old0b")]
+        old_sb = {b: keep.tile([P, T], F32, name="old_sb%d" % b) for b in (1, 2, 3)}
+        retain_quads = placed(AT_QUADS, [P, QUADS_BYTES // 4], F32, "retain_quads")
+        retain_all = placed(AT_RAW0, [P, T], F32, "retain_all")
+        kept0 = [placed(AT_RAW23, [P, EARLY_COLS], F32, "kept0a"), placed(AT_KEPT0B, [P, T - EARLY_COLS], F32, "kept0b")]
+        kept12 = placed(AT_KEPT12, [P, 2 * T], F32, "kept12")
+        late = placed(AT_LATE, [P, 2 * T], F32, "late")
+        kept = {1: kept12[:, 0:T], 2: kept12[:, T:], 3: late[:, 0:T]}
+        result = {b: keep.tile([P, T], F32, name="result%d" % b)[:] for b in (0, 1, 3)}
+        result[2] = late[:, T:]
         ident = keep.tile([P, P], F32, name="ident")
 
         nc.vector.memset(pool_scales[:].bitcast(I32), 0)
         nc.vector.memset(ident[:], 0.0)
         make_identity(nc, ident[:], nomemset=True)
-        nc.vector.memset(retain_rows[:], 0.0)
-        for window in windows[:-1]:
-            nc.vector.memset(window[:], 0.0)
+        nc.vector.memset(window0[:], 0.0)
+        nc.vector.memset(window1[:], 0.0)
 
-        def load_wv(b):
-            nc.sync.dma_start(out=wv_raw[b][:], in_=wv[:, b * P : (b + 1) * P].rearrange("(p j) e -> p j e", j=PACK))
+        def load_wv(dst, lo, hi):
+            nc.sync.dma_start(out=dst, in_=wv[:, lo:hi].rearrange("(p j) e -> p j e", j=PACK))
 
-        def load_old_half(b, h):
-            nc.sync.dma_start(out=old_half[b, h][:], in_=old[b * P : (b + 1) * P, h * BANK : (h + 1) * BANK])
-
-        def load_old(b):
-            nc.sync.dma_start(out=old_sb[b][:], in_=old[b * P : (b + 1) * P, :])
-
-        nc.sync.dma_start(out=retain_octs[:, 0:OCT], in_=retain.rearrange("o (p c) -> (o p) c", c=OCT))
-        load_wv(0)
+        nc.sync.dma_start(
+            out=retain_quads[:, 0 : 2 * LINE].rearrange("p (h c) -> p h c", c=LINE),
+            in_=retain.rearrange("o (h p c) -> p (o h) c", h=2, c=LINE),
+        )
+        load_wv(wv_raw0[:], 0, P)
         nc.sync.dma_start(emb_list[:], offs)
         scale_rows = emb_scales[0].rearrange("(q r) u -> r q u", r=4)
         for r in range(4):
             nc.sync.dma_start(out=pool_scales[r:P:32, :].bitcast(I32), in_=scale_rows[r].bitcast(I32))
         nc.sync.dma_start(out=pool_words[:].bitcast(I32), in_=emb_words[0].bitcast(I32))
-        load_wv(1)
+        load_wv(wv_raw1, P, 2 * P)
         nc.sync.dma_start(place_list[:], offs2)
-        load_old_half(0, 0)
-        load_old_half(0, 1)
-        load_old_half(1, 0)
-        nc.sync.dma_start(out=wv_raw23[:], in_=wv[:, 2 * P :].rearrange("(p j) e -> p j e", j=PACK))
-        load_old_half(1, 1)
-        nc.sync.dma_start(out=retain_rows[0:CHUNKS, :], in_=retain.rearrange("o (c p) -> (o c) p", p=P))
-        for b in range(2, BLOCKS):
-            load_old(b)
+        load_wv(wv_raw23[:], 2 * P, E)
+        nc.sync.dma_start(out=old0[0][:], in_=old[0:P, 0:EARLY_COLS])
+        nc.sync.dma_start(out=old0[1][:], in_=old[0:P, EARLY_COLS:])
+        for b in (1, 2, 3):
+            nc.sync.dma_start(out=old_sb[b][:], in_=old[b * P : (b + 1) * P, :])
 
-        def cast(b):
-            nc.scalar.activation(
-                out=wv_bf[b].rearrange("p (c i j) -> p c j i", i=LINE, j=PACK),
-                in_=wv_src[b].rearrange("p j (c i) -> p c j i", i=LINE),
-                func=COPY,
+        def cast_by_lines(engine_copy, dst, src, lo, hi):
+            engine_copy(
+                out=dst[:, lo * PACK : hi * PACK].rearrange("p (c i j) -> p c j i", i=LINE, j=PACK),
+                in_=src[:, :, lo:hi].rearrange("p j (c i) -> p c j i", i=LINE),
             )
 
-        def project(b, half, dst):
+        def cast_on_gpsimd(dst, src, lo, hi):
+            nc.gpsimd.tensor_scalar(
+                out=dst[:, lo * PACK : hi * PACK].rearrange("p (c j) -> p c j", j=PACK),
+                in0=src[:, :, lo:hi].rearrange("p j c -> p c j"),
+                scalar1=1.0,
+                scalar2=0.0,
+                op0=MULT,
+                op1=ADD,
+            )
+
+        def quantise(src, lo, hi):
+            nc.vector.quantize_mx(out=wv_codes[:, lo:hi].bitcast(FP8X4), scales=wv_scales[:, lo:hi], in_=src[:])
+
+        def project(dst, b, half, lo=0, hi=HALF):
             nc.tensor.matmul_mx(
                 out=dst,
-                lhsT=wv_codes[b].bitcast(FP8X4),
+                lhsT=wv_codes[:, b * P : (b + 1) * P].bitcast(FP8X4),
                 lhsT_scale=wv_scales[:, b * P : (b + 1) * P],
-                rhs=listed_words[half][:].bitcast(FP4X4),
-                rhs_scale=listed_scales[half][:],
+                rhs=listed_words[half][:, lo:hi].bitcast(FP4X4),
+                rhs_scale=listed_scales[half][:, lo:hi],
                 start=True,
                 stop=True,
             )
 
-        def scatter(b, lo, hi, src):
-            nc.vector.tensor_copy(windows[b % WINDOWS][:].indirect(place_list[:, lo // GROUP : hi // GROUP]), src)
+        def places(window, lo, hi):
+            return window[:].indirect(place_list[:, lo // GROUP : hi // GROUP])
 
-        def spread_retain(h, bank):
+        def scatter_on_vector(window, lo, hi, src):
+            nc.vector.tensor_copy(places(window, lo, hi), src)
+
+        def scatter_on_scalar(window, lo, hi, src):
+            nc.scalar.activation(places(window, lo, hi), src, COPY)
+
+        def in_order(bank):
+            return bank[:].rearrange("p (c n) -> p n c", c=LINE)
+
+        def multiply_on_vector(b):
+            for h, bank in enumerate(retain_banks):
+                cols = slice(h * BANK, (h + 1) * BANK)
+                nc.vector.tensor_tensor(
+                    kept[b][:, cols].rearrange("p (n c) -> p n c", c=LINE),
+                    old_sb[b][:, cols].rearrange("p (n c) -> p n c", c=LINE),
+                    in_order(bank),
+                    MULT,
+                )
+
+        def add_and_store(engine, queue, b, src, window, cols):
+            engine.tensor_tensor(result[b][:, cols], src, window[:, cols], ADD)
+            queue.dma_start(out=out[b * P : (b + 1) * P, cols], in_=result[b][:, cols])
+
+        cast_by_lines(nc.vector.tensor_copy, wv_bf0, wv_raw0, 0, VECTOR_COLS)
+        cast_by_lines(nc.scalar.copy, wv_bf0, wv_raw0, VECTOR_COLS, P)
+        for h, bank in enumerate(retain_banks):
             for c in range(LINE):
-                nc.tensor.transpose(bank[:, c * P : (c + 1) * P], retain_octs[:, h * LINE + c : h * LINE + c + 1].to_broadcast([P, P]), ident[:])
-            nc.scalar.copy(out=retain_all[:].rearrange("p (n c) -> p n c", c=OCT)[:, :, h * LINE : (h + 1) * LINE], in_=bank[:].rearrange("p (c n) -> p n c", c=LINE))
-
-        def multiply(b, h):
-            cols = slice(h * BANK, (h + 1) * BANK)
-            nc.gpsimd.tensor_tensor(kept[b][:, cols], old_half[b, h][:], retain_all[:, cols], MULT)
-
-        def add_and_store(b, pieces):
-            for n in range(pieces):
-                cols = slice(n * T // pieces, (n + 1) * T // pieces)
-                nc.gpsimd.tensor_tensor(result[b][:, cols], kept[b][:, cols], windows[b % WINDOWS][:, cols], ADD)
-                nc.sync.dma_start(out=out[b * P : (b + 1) * P, cols], in_=result[b][:, cols])
-
-        def multiply_turned(b, there, back):
-            for h in range(T // BANK):
-                for c in range(BANK // P):
-                    col = h * BANK + c * P
-                    nc.tensor.transpose(there[h][:, c * P : (c + 1) * P], old_sb[b][:, col : col + P], ident[:])
-                for c in range(BANK // P):
-                    chunk = h * BANK // P + c
-                    nc.scalar.activation(out=turned[b % 2][:, chunk], in_=there[h][:, c * P : (c + 1) * P], func=COPY, scale=retain_cols[:, chunk : chunk + 1])
-            for chunk in range(CHUNKS):
-                h, c = divmod(chunk, BANK // P)
-                nc.tensor.transpose(back[h][:, c * P : (c + 1) * P], turned[b % 2][:, chunk], ident[:])
-
-        for engine_copy, cols in ((nc.vector.tensor_copy, slice(0, VECTOR_COLS)), (nc.scalar.copy, slice(VECTOR_COLS, P))):
-            engine_copy(
-                out=wv_bf[0][:, cols.start * PACK : cols.stop * PACK].rearrange("p (c i j) -> p c j i", i=LINE, j=PACK),
-                in_=wv_src[0][:, :, cols].rearrange("p j (c i) -> p c j i", i=LINE),
-            )
-        spread_retain(0, banks[0])
-        spread_retain(1, banks[1])
+                col = h * LINE + c
+                nc.tensor.transpose(bank[:, c * P : (c + 1) * P], retain_quads[:, col : col + 1].to_broadcast([P, P]), ident[:])
+            nc.scalar.copy(out=retain_all[:, h * BANK : (h + 1) * BANK].rearrange("p (n c) -> p n c", c=LINE), in_=in_order(bank))
 
         half_lists = [emb_list[:, 0 : HALF // GROUP], emb_list[:, HALF // GROUP :]]
         nc.vector.tensor_copy(listed_scales[0][:], pool_scales[:].indirect(half_lists[0]))
-        nc.vector.quantize_mx(out=codes0[:].bitcast(FP8X4), scales=wv_scales[:, 0:P], in_=wv_bf0[:])
-        nc.gpsimd.memset(windows[-1][:], 0.0)
+        quantise(wv_bf0, 0, P)
+        nc.gpsimd.memset(window2[:], 0.0)
         for half in range(2):
             nc.vector.tensor_copy(listed_words[half][:], pool_words[:].indirect(half_lists[half]))
+        cast_on_gpsimd(wv_bf1, wv_raw1, 0, P // 2)
+        cast_by_lines(nc.scalar.copy, wv_bf1, wv_raw1, P // 2, P)
+        quantise(wv_bf1, P, 2 * P)
         nc.vector.tensor_copy(listed_scales[1][:], pool_scales[:].indirect(half_lists[1]))
-        nc.gpsimd.tensor_scalar(
-            out=wv_bf1[:, 0 : P // 2 * PACK].rearrange("p (c j) -> p c j", j=PACK),
-            in0=wv_raw[1][:, :, 0 : P // 2].rearrange("p j c -> p c j"),
-            scalar1=1.0,
-            scalar2=0.0,
-            op0=MULT,
-            op1=ADD,
-        )
-        nc.scalar.copy(
-            out=wv_bf1[:, P // 2 * PACK :].rearrange("p (c i j) -> p c j i", i=LINE, j=PACK),
-            in_=wv_raw[1][:, :, P // 2 :].rearrange("p j (c i) -> p c j i", i=LINE),
-        )
-        nc.vector.quantize_mx(out=wv_codes[1].bitcast(FP8X4), scales=wv_scales[:, P : 2 * P], in_=wv_bf1[:])
 
-        def half_step(b, half, bank):
-            project(b, half, bank[:, 0:HALF])
-            nc.scalar.copy(out=values[b, half][:], in_=bank[:, 0:HALF])
-            scatter(b, half * HALF, (half + 1) * HALF, values[b, half][:])
+        for n, bank in enumerate(banks[2:4]):
+            project(bank[:, 0:P], 0, 0, n * P, (n + 1) * P)
+            nc.scalar.copy(out=first0[:, n * P : (n + 1) * P], in_=bank[:, 0:P])
+        scatter_on_scalar(window0, 0, HALF, first0[:])
+        project(banks[4][:, 0:HALF], 1, 0)
+        nc.vector.tensor_copy(first1[:], banks[4][:, 0:HALF])
+        scatter_on_vector(window1, 0, HALF, first1[:])
+        project(banks[4][:, HALF:], 0, 1)
+        nc.scalar.copy(out=second0[:], in_=banks[4][:, HALF:])
+        scatter_on_scalar(window0, HALF, I, second0[:])
+        project(banks[2][:, 0:HALF], 1, 1)
 
-        for n, bank in enumerate(banks[0:2]):
-            cols = slice(n * P, (n + 1) * P)
-            nc.tensor.matmul_mx(
-                out=bank[:, 0:P],
-                lhsT=wv_codes[0].bitcast(FP8X4),
-                lhsT_scale=wv_scales[:, 0:P],
-                rhs=listed_words[0][:, cols].bitcast(FP4X4),
-                rhs_scale=listed_scales[0][:, cols],
-                start=True,
-                stop=True,
-            )
-            nc.scalar.copy(out=values[0, 0][:, cols], in_=bank[:, 0:P])
-        scatter(0, 0, HALF, values[0, 0][:])
-        project(1, 0, banks[1][:, 0:HALF])
-        nc.scalar.copy(out=values[1][:, 0:HALF], in_=banks[1][:, 0:HALF])
-        scatter(1, 0, FIRST1, values[1][:, 0:FIRST1])
-        half_step(0, 1, banks[1])
-        multiply(0, 0)
-        multiply(0, 1)
-        multiply(1, 0)
-        cast(2)
-        cast(3)
-        nc.vector.quantize_mx(out=codes123[:, P:].bitcast(FP8X4), scales=wv_scales[:, 2 * P :], in_=wv_bf23[:])
-        project(1, 1, banks[1][:, 0:HALF])
-        nc.scalar.copy(out=values[1][:, HALF:], in_=banks[1][:, 0:HALF])
-        scatter(1, FIRST1, I, values[1][:, FIRST1:])
-        for half in range(2):
-            project(2, half, banks[2 + half][:, 0:HALF])
-            nc.scalar.copy(out=values[2][:, half * HALF : (half + 1) * HALF], in_=banks[2 + half][:, 0:HALF])
-        for half in range(2):
-            project(3, half, banks[4][:, half * HALF : (half + 1) * HALF])
-        nc.scalar.copy(out=values[3][:], in_=banks[4][:])
-        add_and_store(0, 1)
-        multiply(1, 1)
-        add_and_store(1, 1)
+        for n in range(2):
+            cast_on_gpsimd(wv_bf23, wv_raw23, n * P, (n + 1) * P)
+        nc.gpsimd.tensor_tensor(kept0[0][:], old0[0][:], retain_all[:, 0:EARLY_COLS], MULT)
+        quantise(wv_bf23, 2 * P, E)
+        nc.vector.tensor_copy(second1[:], banks[2][:, 0:HALF])
+        scatter_on_vector(window1, HALF, I, second1[:])
+        nc.gpsimd.tensor_tensor(kept0[1][:], old0[1][:], retain_all[:, EARLY_COLS:], MULT)
 
-        nc.tensor.transpose(banks[1][:, 0:P], retain_rows[:], ident[:])
-        nc.scalar.copy(out=retain_cols[:], in_=banks[1][:, 0:CHUNKS])
-        multiply_turned(2, banks[0:2], banks[4:6])
-        for h in range(T // BANK):
-            nc.scalar.copy(out=kept[2][:, h * BANK : (h + 1) * BANK], in_=banks[4 + h][:])
-        multiply_turned(3, [banks[2], banks[3]], banks[6:8])
-        nc.scalar.copy(out=kept_end[:], in_=banks[7][:, BANK - POOL_END :])
+        for b in (2, 3):
+            for half in range(2):
+                project(banks[4 + b][:, half * HALF : (half + 1) * HALF], b, half)
+        nc.scalar.copy(out=values2[:], in_=banks[6][:])
+        nc.scalar.copy(out=values3[:, 0:VECTOR_SLOTS3], in_=banks[7][:, 0:VECTOR_SLOTS3])
+        scatter_on_scalar(window2, 0, HALF, values2[:, 0:HALF])
+        nc.scalar.copy(out=values3[:, VECTOR_SLOTS3:], in_=banks[7][:, VECTOR_SLOTS3:])
+        scatter_on_scalar(window2, HALF, I, values2[:, HALF:])
 
-        scatter(2, 0, I, values[2][:])
-        add_and_store(2, 2)
-        last = BLOCKS - 1
-        scatter(last, 0, I, values[last][:])
-        window = windows[last % WINDOWS]
-        edges = [0, QUARTER, BANK, T - POOL_END, T]
-        for n in range(4):
-            cols = slice(edges[n], edges[n + 1])
-            if n < 3:
-                h, c = divmod(edges[n], BANK)
-                nc.vector.tensor_tensor(result[last][:, cols], banks[6 + h][:, c : c + edges[n + 1] - edges[n]], window[:, cols], ADD)
-            else:
-                nc.gpsimd.tensor_tensor(result[last][:, cols], kept_end[:], window[:, cols], ADD)
-            nc.sync.dma_start(out=out[last * P :, cols], in_=result[last][:, cols])
+        multiply_on_vector(1)
+        multiply_on_vector(2)
+        add_and_store(nc.gpsimd, nc.sync, 0, kept0[0][:], window0, slice(0, EARLY_COLS))
+        add_and_store(nc.gpsimd, nc.sync, 0, kept0[1][:], window0, slice(EARLY_COLS, T))
+        for h in range(2):
+            cols = slice(h * BANK, (h + 1) * BANK)
+            add_and_store(nc.gpsimd, nc.sync, 1, kept[1][:, cols], window1, cols)
+
+        scatter_on_vector(window0, 0, VECTOR_SLOTS3, values3[:, 0:VECTOR_SLOTS3])
+        scatter_on_scalar(window0, VECTOR_SLOTS3, I, values3[:, VECTOR_SLOTS3:])
+        multiply_on_vector(3)
+        for b, window, pieces in ((2, window2, 2), (3, window0, 4)):
+            for n in range(pieces):
+                cols = slice(n * T // pieces, (n + 1) * T // pieces)
+                add_and_store(nc.vector, nc.scalar, b, kept[b][:, cols], window, cols)

@@ -164,18 +164,10 @@ def tile_attend_cachewrite_kernel(tc, emb_words, emb_scales, wv, old, retain, of
         def scatter_on_scalar(window, lo, hi, src):
             nc.scalar.activation(places(window, lo, hi), src, COPY)
 
-        def in_order(bank):
-            return bank[:].rearrange("p (c n) -> p n c", c=LINE)
-
         def multiply_on_vector(b):
             for h, bank in enumerate(retain_banks):
                 cols = slice(h * BANK, (h + 1) * BANK)
-                nc.vector.tensor_tensor(
-                    kept[b][:, cols].rearrange("p (n c) -> p n c", c=LINE),
-                    old_sb[b][:, cols].rearrange("p (n c) -> p n c", c=LINE),
-                    in_order(bank),
-                    MULT,
-                )
+                nc.vector.tensor_tensor(kept[b][:, cols], old_sb[b][:, cols], bank[:], MULT)
 
         def add_and_store(engine, queue, b, src, window, cols):
             engine.tensor_tensor(result[b][:, cols], src, window[:, cols], ADD)
@@ -186,8 +178,8 @@ def tile_attend_cachewrite_kernel(tc, emb_words, emb_scales, wv, old, retain, of
         for h, bank in enumerate(retain_banks):
             for c in range(LINE):
                 col = h * LINE + c
-                nc.tensor.transpose(bank[:, c * P : (c + 1) * P], retain_quads[:, col : col + 1].to_broadcast([P, P]), ident[:])
-            nc.scalar.copy(out=retain_all[:, h * BANK : (h + 1) * BANK].rearrange("p (n c) -> p n c", c=LINE), in_=in_order(bank))
+                nc.tensor.transpose(bank[:, c:BANK:LINE], retain_quads[:, col : col + 1].to_broadcast([P, P]), ident[:])
+            nc.scalar.copy(out=retain_all[:, h * BANK : (h + 1) * BANK], in_=bank[:])
 
         half_lists = [emb_list[:, 0 : HALF // GROUP], emb_list[:, HALF // GROUP :]]
         nc.vector.tensor_copy(listed_scales[0][:], pool_scales[:].indirect(half_lists[0]))

@@ -27,23 +27,24 @@ GROUP = 16
 ALIGN = 64
 KIB = 1024
 VECTOR_COLS = 96
-EARLY_COLS = 512
-VECTOR_SLOTS3 = 256
+EARLY_COLS = 448
+VECTOR_SLOTS3 = 160
 
 AT_BF1 = 0
 AT_WORDS0 = AT_BF1 + KIB
 AT_WORDS1 = AT_WORDS0 + 2 * HALF
 AT_QUADS = AT_WORDS0 - ALIGN
 QUADS_BYTES = AT_WORDS1 + ALIGN - AT_QUADS
-AT_BF0 = 4 * KIB
+AT_BF0 = 44 * KIB
 AT_RAW0 = 8 * KIB
 AT_RAW23 = 12 * KIB
 AT_KEPT12 = 16 * KIB
-AT_BF23 = AT_KEPT12 + 8 * KIB - ALIGN
+AT_BF23 = AT_KEPT12 + 6 * KIB - ALIGN
 AT_KEPT0B = AT_BF23 + 2 * KIB - ALIGN
 AT_LATE = AT_KEPT0B + 4 * (T - EARLY_COLS) - ALIGN
-AT_SCALES1 = AT_LATE + 8 * KIB
+AT_SCALES1 = AT_LATE + 10 * KIB
 AT_RAW1 = AT_BF23
+AT_KEPT0A = AT_BF23 + ALIGN
 RAW1_BYTES = AT_SCALES1 + ALIGN - AT_RAW1
 
 
@@ -77,9 +78,8 @@ def tile_attend_cachewrite_kernel(tc, emb_words, emb_scales, wv, old, retain, of
         wv_scales = keep.tile([P, E], U8, name="wv_scales", align_bytes=ALIGN)
 
         first0 = keep.tile([P, HALF], F32, name="first0")
-        first1 = keep.tile([P, HALF], F32, name="first1")
+        values1 = keep.tile([P, I], F32, name="values1")
         second0 = keep.tile([P, HALF], F32, name="second0")
-        second1 = placed(AT_RAW23 + 4 * EARLY_COLS, [P, HALF], F32, "second1")
         values2 = keep.tile([P, I], F32, name="values2")
         values3 = keep.tile([P, I], F32, name="values3")
         window0 = keep.tile([P, T], F32, name="window0")
@@ -90,12 +90,17 @@ def tile_attend_cachewrite_kernel(tc, emb_words, emb_scales, wv, old, retain, of
         old_sb = {b: keep.tile([P, T], F32, name="old_sb%d" % b) for b in (1, 2, 3)}
         retain_quads = placed(AT_QUADS, [P, QUADS_BYTES // 4], F32, "retain_quads")
         retain_all = placed(AT_RAW0, [P, T], F32, "retain_all")
-        kept0 = [placed(AT_RAW23, [P, EARLY_COLS], F32, "kept0a"), placed(AT_KEPT0B, [P, T - EARLY_COLS], F32, "kept0b")]
-        kept12 = placed(AT_KEPT12, [P, 2 * T], F32, "kept12")
-        late = placed(AT_LATE, [P, 2 * T], F32, "late")
-        kept = {1: kept12[:, 0:T], 2: kept12[:, T:], 3: late[:, 0:T]}
+        kept0 = [placed(AT_KEPT0A, [P, EARLY_COLS], F32, "kept0a"), placed(AT_KEPT0B, [P, T - EARLY_COLS], F32, "kept0b")]
+        kept12 = placed(AT_KEPT12, [P, 3 * BANK], F32, "kept12")
+        late = placed(AT_LATE, [P, 5 * BANK], F32, "late")
+        kept_halves = [kept12[:, n * BANK : (n + 1) * BANK] for n in range(3)] + [late[:, n * BANK : (n + 1) * BANK] for n in range(3)]
+
+        def kept(b, cols):
+            h = cols.start // BANK
+            return kept_halves[2 * (b - 1) + h][:, cols.start - h * BANK : cols.stop - h * BANK]
+
         result = {b: keep.tile([P, T], F32, name="result%d" % b)[:] for b in (0, 1, 3)}
-        result[2] = late[:, T:]
+        result[2] = late[:, 3 * BANK :]
         ident = keep.tile([P, P], F32, name="ident")
 
         nc.vector.memset(pool_scales[:].bitcast(I32), 0)
@@ -164,10 +169,9 @@ def tile_attend_cachewrite_kernel(tc, emb_words, emb_scales, wv, old, retain, of
         def scatter_on_scalar(window, lo, hi, src):
             nc.scalar.activation(places(window, lo, hi), src, COPY)
 
-        def multiply_on_vector(b):
-            for h, bank in enumerate(retain_banks):
-                cols = slice(h * BANK, (h + 1) * BANK)
-                nc.vector.tensor_tensor(kept[b][:, cols], old_sb[b][:, cols], bank[:], MULT)
+        def multiply_on_vector(b, h):
+            cols = slice(h * BANK, (h + 1) * BANK)
+            nc.vector.tensor_tensor(kept(b, cols), old_sb[b][:, cols], retain_banks[h][:], MULT)
 
         def add_and_store(engine, queue, b, src, window, cols):
             engine.tensor_tensor(result[b][:, cols], src, window[:, cols], ADD)
@@ -196,20 +200,17 @@ def tile_attend_cachewrite_kernel(tc, emb_words, emb_scales, wv, old, retain, of
             project(bank[:, 0:P], 0, 0, n * P, (n + 1) * P)
             nc.scalar.copy(out=first0[:, n * P : (n + 1) * P], in_=bank[:, 0:P])
         scatter_on_scalar(window0, 0, HALF, first0[:])
-        project(banks[4][:, 0:HALF], 1, 0)
-        nc.vector.tensor_copy(first1[:], banks[4][:, 0:HALF])
-        scatter_on_vector(window1, 0, HALF, first1[:])
-        project(banks[4][:, HALF:], 0, 1)
-        nc.scalar.copy(out=second0[:], in_=banks[4][:, HALF:])
-        scatter_on_scalar(window0, HALF, I, second0[:])
-        project(banks[2][:, 0:HALF], 1, 1)
-
-        for n in range(2):
-            cast_on_gpsimd(wv_bf23, wv_raw23, n * P, (n + 1) * P)
-        nc.gpsimd.tensor_tensor(kept0[0][:], old0[0][:], retain_all[:, 0:EARLY_COLS], MULT)
+        for half in range(2):
+            project(banks[4][:, half * HALF : (half + 1) * HALF], 1, half)
+        cast_by_lines(nc.vector.tensor_copy, wv_bf23, wv_raw23, 0, 2 * P)
+        nc.vector.tensor_copy(values1[:], banks[4][:])
         quantise(wv_bf23, 2 * P, E)
-        nc.vector.tensor_copy(second1[:], banks[2][:, 0:HALF])
-        scatter_on_vector(window1, HALF, I, second1[:])
+        scatter_on_vector(window1, 0, I, values1[:])
+        project(banks[3][:, 0:HALF], 0, 1)
+        nc.scalar.copy(out=second0[:], in_=banks[3][:, 0:HALF])
+        scatter_on_scalar(window0, HALF, I, second0[:])
+
+        nc.gpsimd.tensor_tensor(kept0[0][:], old0[0][:], retain_all[:, 0:EARLY_COLS], MULT)
         nc.gpsimd.tensor_tensor(kept0[1][:], old0[1][:], retain_all[:, EARLY_COLS:], MULT)
 
         for b in (2, 3):
@@ -221,18 +222,19 @@ def tile_attend_cachewrite_kernel(tc, emb_words, emb_scales, wv, old, retain, of
         nc.scalar.copy(out=values3[:, VECTOR_SLOTS3:], in_=banks[7][:, VECTOR_SLOTS3:])
         scatter_on_scalar(window2, HALF, I, values2[:, HALF:])
 
-        multiply_on_vector(1)
-        multiply_on_vector(2)
+        for b, h in ((1, 0), (1, 1), (2, 0)):
+            multiply_on_vector(b, h)
         add_and_store(nc.gpsimd, nc.sync, 0, kept0[0][:], window0, slice(0, EARLY_COLS))
         add_and_store(nc.gpsimd, nc.sync, 0, kept0[1][:], window0, slice(EARLY_COLS, T))
         for h in range(2):
             cols = slice(h * BANK, (h + 1) * BANK)
-            add_and_store(nc.gpsimd, nc.sync, 1, kept[1][:, cols], window1, cols)
+            add_and_store(nc.gpsimd, nc.sync, 1, kept(1, cols), window1, cols)
 
         scatter_on_vector(window0, 0, VECTOR_SLOTS3, values3[:, 0:VECTOR_SLOTS3])
         scatter_on_scalar(window0, VECTOR_SLOTS3, I, values3[:, VECTOR_SLOTS3:])
-        multiply_on_vector(3)
+        for b, h in ((2, 1), (3, 0), (3, 1)):
+            multiply_on_vector(b, h)
         for b, window, pieces in ((2, window2, 2), (3, window0, 4)):
             for n in range(pieces):
                 cols = slice(n * T // pieces, (n + 1) * T // pieces)
-                add_and_store(nc.vector, nc.scalar, b, kept[b][:, cols], window, cols)
+                add_and_store(nc.vector, nc.scalar, b, kept(b, cols), window, cols)

@@ -27,24 +27,22 @@ GROUP = 16
 ALIGN = 64
 KIB = 1024
 VECTOR_COLS = 96
-EARLY_COLS = 448
-VECTOR_SLOTS3 = 160
+VECTOR_SLOTS3 = 224
 
 AT_BF1 = 0
 AT_WORDS0 = AT_BF1 + KIB
 AT_WORDS1 = AT_WORDS0 + 2 * HALF
 AT_QUADS = AT_WORDS0 - ALIGN
 QUADS_BYTES = AT_WORDS1 + ALIGN - AT_QUADS
-AT_BF0 = 44 * KIB
+AT_BF0 = 48 * KIB
+AT_OLD0 = 52 * KIB
 AT_RAW0 = 8 * KIB
-AT_RAW23 = 12 * KIB
 AT_KEPT12 = 16 * KIB
 AT_BF23 = AT_KEPT12 + 6 * KIB - ALIGN
-AT_KEPT0B = AT_BF23 + 2 * KIB - ALIGN
-AT_LATE = AT_KEPT0B + 4 * (T - EARLY_COLS) - ALIGN
+AT_KEPT0 = AT_BF23 + 2 * KIB - ALIGN
+AT_LATE = AT_KEPT0 + 4 * KIB - ALIGN
 AT_SCALES1 = AT_LATE + 10 * KIB
 AT_RAW1 = AT_BF23
-AT_KEPT0A = AT_BF23 + ALIGN
 RAW1_BYTES = AT_SCALES1 + ALIGN - AT_RAW1
 
 
@@ -70,27 +68,26 @@ def tile_attend_cachewrite_kernel(tc, emb_words, emb_scales, wv, old, retain, of
 
         wv_raw0 = placed(AT_RAW0, [P, PACK, P], F32, "wv_raw0")
         wv_raw1 = placed(AT_RAW1, [P, RAW1_BYTES // 4], F32, "wv_raw1")[:, 0 : PACK * P].rearrange("p (j e) -> p j e", j=PACK)
-        wv_raw23 = placed(AT_RAW23, [P, PACK, 2 * P], F32, "wv_raw23")
+        wv_raw23 = keep.tile([P, PACK, 2 * P], F32, name="wv_raw23")
         wv_bf0 = placed(AT_BF0, [P, P * PACK], BF16, "wv_bf0")
         wv_bf1 = placed(AT_BF1, [P, P * PACK], BF16, "wv_bf1")
         wv_bf23 = placed(AT_BF23, [P, 2 * P * PACK], BF16, "wv_bf23")
         wv_codes = keep.tile([P, E], U32, name="wv_codes", align_bytes=ALIGN)
         wv_scales = keep.tile([P, E], U8, name="wv_scales", align_bytes=ALIGN)
 
-        first0 = keep.tile([P, HALF], F32, name="first0")
+        values0 = keep.tile([P, I], F32, name="values0")
         values1 = keep.tile([P, I], F32, name="values1")
-        second0 = keep.tile([P, HALF], F32, name="second0")
         values2 = keep.tile([P, I], F32, name="values2")
         values3 = keep.tile([P, I], F32, name="values3")
         window0 = keep.tile([P, T], F32, name="window0")
         window1 = keep.tile([P, T], F32, name="window1")
         window2 = placed(AT_BF0, [P, T], F32, "window2")
+        window3 = keep.tile([P, T], F32, name="window3")
 
-        old0 = [keep.tile([P, EARLY_COLS], F32, name="old0a"), keep.tile([P, T - EARLY_COLS], F32, name="old0b")]
-        old_sb = {b: keep.tile([P, T], F32, name="old_sb%d" % b) for b in (1, 2, 3)}
+        old_sb = [placed(AT_OLD0, [P, T], F32, "old_sb0")] + [keep.tile([P, T], F32, name="old_sb%d" % b) for b in (1, 2, 3)]
         retain_quads = placed(AT_QUADS, [P, QUADS_BYTES // 4], F32, "retain_quads")
         retain_all = placed(AT_RAW0, [P, T], F32, "retain_all")
-        kept0 = [placed(AT_KEPT0A, [P, EARLY_COLS], F32, "kept0a"), placed(AT_KEPT0B, [P, T - EARLY_COLS], F32, "kept0b")]
+        kept0 = placed(AT_KEPT0, [P, T], F32, "kept0")
         kept12 = placed(AT_KEPT12, [P, 3 * BANK], F32, "kept12")
         late = placed(AT_LATE, [P, 5 * BANK], F32, "late")
         kept_halves = [kept12[:, n * BANK : (n + 1) * BANK] for n in range(3)] + [late[:, n * BANK : (n + 1) * BANK] for n in range(3)]
@@ -99,11 +96,13 @@ def tile_attend_cachewrite_kernel(tc, emb_words, emb_scales, wv, old, retain, of
             h = cols.start // BANK
             return kept_halves[2 * (b - 1) + h][:, cols.start - h * BANK : cols.stop - h * BANK]
 
-        result = {b: keep.tile([P, T], F32, name="result%d" % b)[:] for b in (0, 1, 3)}
+        result = {b: keep.tile([P, T], F32, name="result%d" % b)[:] for b in (0, 3)}
+        result[1] = placed(AT_OLD0, [P, T], F32, "result1")[:]
         result[2] = late[:, 3 * BANK :]
         ident = keep.tile([P, P], F32, name="ident")
 
-        nc.vector.memset(pool_scales[:].bitcast(I32), 0)
+        nc.gpsimd.memset(pool_scales[:].bitcast(I32), 0)
+        nc.gpsimd.memset(window3[:], 0.0)
         nc.vector.memset(ident[:], 0.0)
         make_identity(nc, ident[:], nomemset=True)
         nc.vector.memset(window0[:], 0.0)
@@ -125,9 +124,7 @@ def tile_attend_cachewrite_kernel(tc, emb_words, emb_scales, wv, old, retain, of
         load_wv(wv_raw1, P, 2 * P)
         nc.sync.dma_start(place_list[:], offs2)
         load_wv(wv_raw23[:], 2 * P, E)
-        nc.sync.dma_start(out=old0[0][:], in_=old[0:P, 0:EARLY_COLS])
-        nc.sync.dma_start(out=old0[1][:], in_=old[0:P, EARLY_COLS:])
-        for b in (1, 2, 3):
+        for b in range(4):
             nc.sync.dma_start(out=old_sb[b][:], in_=old[b * P : (b + 1) * P, :])
 
         def cast_by_lines(engine_copy, dst, src, lo, hi):
@@ -198,8 +195,8 @@ def tile_attend_cachewrite_kernel(tc, emb_words, emb_scales, wv, old, retain, of
 
         for n, bank in enumerate(banks[2:4]):
             project(bank[:, 0:P], 0, 0, n * P, (n + 1) * P)
-            nc.scalar.copy(out=first0[:, n * P : (n + 1) * P], in_=bank[:, 0:P])
-        scatter_on_scalar(window0, 0, HALF, first0[:])
+            nc.scalar.copy(out=values0[:, n * P : (n + 1) * P], in_=bank[:, 0:P])
+        scatter_on_scalar(window0, 0, P, values0[:, 0:P])
         for half in range(2):
             project(banks[4][:, half * HALF : (half + 1) * HALF], 1, half)
         cast_by_lines(nc.vector.tensor_copy, wv_bf23, wv_raw23, 0, 2 * P)
@@ -207,11 +204,10 @@ def tile_attend_cachewrite_kernel(tc, emb_words, emb_scales, wv, old, retain, of
         quantise(wv_bf23, 2 * P, E)
         scatter_on_vector(window1, 0, I, values1[:])
         project(banks[3][:, 0:HALF], 0, 1)
-        nc.scalar.copy(out=second0[:], in_=banks[3][:, 0:HALF])
-        scatter_on_scalar(window0, HALF, I, second0[:])
+        nc.scalar.copy(out=values0[:, HALF:], in_=banks[3][:, 0:HALF])
+        scatter_on_scalar(window0, P, I, values0[:, P:])
 
-        nc.gpsimd.tensor_tensor(kept0[0][:], old0[0][:], retain_all[:, 0:EARLY_COLS], MULT)
-        nc.gpsimd.tensor_tensor(kept0[1][:], old0[1][:], retain_all[:, EARLY_COLS:], MULT)
+        nc.gpsimd.tensor_tensor(kept0[:], old_sb[0][:], retain_all[:], MULT)
 
         for b in (2, 3):
             for half in range(2):
@@ -222,19 +218,18 @@ def tile_attend_cachewrite_kernel(tc, emb_words, emb_scales, wv, old, retain, of
         nc.scalar.copy(out=values3[:, VECTOR_SLOTS3:], in_=banks[7][:, VECTOR_SLOTS3:])
         scatter_on_scalar(window2, HALF, I, values2[:, HALF:])
 
+        scatter_on_vector(window3, 0, VECTOR_SLOTS3, values3[:, 0:VECTOR_SLOTS3])
         for b, h in ((1, 0), (1, 1), (2, 0)):
             multiply_on_vector(b, h)
-        add_and_store(nc.gpsimd, nc.sync, 0, kept0[0][:], window0, slice(0, EARLY_COLS))
-        add_and_store(nc.gpsimd, nc.sync, 0, kept0[1][:], window0, slice(EARLY_COLS, T))
+        add_and_store(nc.gpsimd, nc.sync, 0, kept0[:], window0, slice(0, T))
         for h in range(2):
             cols = slice(h * BANK, (h + 1) * BANK)
             add_and_store(nc.gpsimd, nc.sync, 1, kept(1, cols), window1, cols)
 
-        scatter_on_vector(window0, 0, VECTOR_SLOTS3, values3[:, 0:VECTOR_SLOTS3])
-        scatter_on_scalar(window0, VECTOR_SLOTS3, I, values3[:, VECTOR_SLOTS3:])
+        scatter_on_scalar(window3, VECTOR_SLOTS3, I, values3[:, VECTOR_SLOTS3:])
         for b, h in ((2, 1), (3, 0), (3, 1)):
             multiply_on_vector(b, h)
-        for b, window, pieces in ((2, window2, 2), (3, window0, 4)):
+        for b, window, pieces in ((2, window2, 2), (3, window3, 4)):
             for n in range(pieces):
                 cols = slice(n * T // pieces, (n + 1) * T // pieces)
                 add_and_store(nc.vector, nc.scalar, b, kept(b, cols), window, cols)

@@ -101,12 +101,12 @@ def tile_attend_cachewrite_kernel(tc, emb_words, emb_scales, wv, old, retain, of
         result[2] = late[:, 3 * BANK :]
         ident = keep.tile([P, P], F32, name="ident")
 
-        nc.gpsimd.memset(pool_scales[:].bitcast(I32), 0)
-        nc.gpsimd.memset(window3[:], 0.0)
+        nc.vector.memset(pool_scales[:].bitcast(I32), 0)
         nc.vector.memset(ident[:], 0.0)
         make_identity(nc, ident[:], nomemset=True)
         nc.vector.memset(window0[:], 0.0)
         nc.vector.memset(window1[:], 0.0)
+        nc.vector.memset(window3[:], 0.0)
 
         def load_wv(dst, lo, hi):
             nc.sync.dma_start(out=dst, in_=wv[:, lo:hi].rearrange("(p j) e -> p j e", j=PACK))

@@ -26,7 +26,7 @@ HALF = I // 2
 GROUP = 16
 ALIGN = 64
 KIB = 1024
-VECTOR_COLS = 96
+GPSIMD_COLS = 32
 VECTOR_SLOTS3 = 224
 
 AT_BF1 = 0
@@ -36,7 +36,6 @@ AT_QUADS = AT_WORDS0 - ALIGN
 QUADS_BYTES = AT_WORDS1 + ALIGN - AT_QUADS
 AT_BF0 = 48 * KIB
 AT_OLD0 = 52 * KIB
-AT_RAW0 = 8 * KIB
 AT_KEPT12 = 16 * KIB
 AT_BF23 = AT_KEPT12 + 6 * KIB - ALIGN
 AT_KEPT0 = AT_BF23 + 2 * KIB - ALIGN
@@ -66,7 +65,7 @@ def tile_attend_cachewrite_kernel(tc, emb_words, emb_scales, wv, old, retain, of
         listed_words = [placed(AT_WORDS0, [P, HALF], U16, "listed_words0"), placed(AT_WORDS1, [P, HALF], U16, "listed_words1")]
         listed_scales = [keep.tile([P, HALF], U8, name="listed_scales0", align_bytes=ALIGN), placed(AT_SCALES1, [P, HALF], U8, "listed_scales1")]
 
-        wv_raw0 = placed(AT_RAW0, [P, PACK, P], F32, "wv_raw0")
+        wv_raw0 = keep.tile([P, PACK, P], F32, name="wv_raw0")
         wv_raw1 = placed(AT_RAW1, [P, RAW1_BYTES // 4], F32, "wv_raw1")[:, 0 : PACK * P].rearrange("p (j e) -> p j e", j=PACK)
         wv_raw23 = keep.tile([P, PACK, 2 * P], F32, name="wv_raw23")
         wv_bf0 = placed(AT_BF0, [P, P * PACK], BF16, "wv_bf0")
@@ -86,7 +85,7 @@ def tile_attend_cachewrite_kernel(tc, emb_words, emb_scales, wv, old, retain, of
 
         old_sb = [placed(AT_OLD0, [P, T], F32, "old_sb0")] + [keep.tile([P, T], F32, name="old_sb%d" % b) for b in (1, 2, 3)]
         retain_quads = placed(AT_QUADS, [P, QUADS_BYTES // 4], F32, "retain_quads")
-        retain_all = placed(AT_RAW0, [P, T], F32, "retain_all")
+        retain_all = keep.tile([P, T], F32, name="retain_all")
         kept0 = placed(AT_KEPT0, [P, T], F32, "kept0")
         kept12 = placed(AT_KEPT12, [P, 3 * BANK], F32, "kept12")
         late = placed(AT_LATE, [P, 5 * BANK], F32, "late")
@@ -166,21 +165,26 @@ def tile_attend_cachewrite_kernel(tc, emb_words, emb_scales, wv, old, retain, of
         def scatter_on_scalar(window, lo, hi, src):
             nc.scalar.activation(places(window, lo, hi), src, COPY)
 
+        def by_lines(cols):
+            return cols.rearrange("p (n c) -> p n c", c=LINE)
+
+        def in_order(bank):
+            return bank[:].rearrange("p (c n) -> p n c", c=LINE)
+
         def multiply_on_vector(b, h):
             cols = slice(h * BANK, (h + 1) * BANK)
-            nc.vector.tensor_tensor(kept(b, cols), old_sb[b][:, cols], retain_banks[h][:], MULT)
+            nc.vector.tensor_tensor(by_lines(kept(b, cols)), by_lines(old_sb[b][:, cols]), in_order(retain_banks[h]), MULT)
 
         def add_and_store(engine, queue, b, src, window, cols):
             engine.tensor_tensor(result[b][:, cols], src, window[:, cols], ADD)
             queue.dma_start(out=out[b * P : (b + 1) * P, cols], in_=result[b][:, cols])
 
-        cast_by_lines(nc.vector.tensor_copy, wv_bf0, wv_raw0, 0, VECTOR_COLS)
-        cast_by_lines(nc.scalar.copy, wv_bf0, wv_raw0, VECTOR_COLS, P)
+        cast_by_lines(nc.vector.tensor_copy, wv_bf0, wv_raw0, 0, P)
         for h, bank in enumerate(retain_banks):
             for c in range(LINE):
                 col = h * LINE + c
-                nc.tensor.transpose(bank[:, c:BANK:LINE], retain_quads[:, col : col + 1].to_broadcast([P, P]), ident[:])
-            nc.scalar.copy(out=retain_all[:, h * BANK : (h + 1) * BANK], in_=bank[:])
+                nc.tensor.transpose(bank[:, c * P : (c + 1) * P], retain_quads[:, col : col + 1].to_broadcast([P, P]), ident[:])
+            nc.scalar.copy(out=by_lines(retain_all[:, h * BANK : (h + 1) * BANK]), in_=in_order(bank))
 
         half_lists = [emb_list[:, 0 : HALF // GROUP], emb_list[:, HALF // GROUP :]]
         nc.vector.tensor_copy(listed_scales[0][:], pool_scales[:].indirect(half_lists[0]))
@@ -188,8 +192,8 @@ def tile_attend_cachewrite_kernel(tc, emb_words, emb_scales, wv, old, retain, of
         nc.gpsimd.memset(window2[:], 0.0)
         for half in range(2):
             nc.vector.tensor_copy(listed_words[half][:], pool_words[:].indirect(half_lists[half]))
-        cast_on_gpsimd(wv_bf1, wv_raw1, 0, P // 2)
-        cast_by_lines(nc.scalar.copy, wv_bf1, wv_raw1, P // 2, P)
+        cast_on_gpsimd(wv_bf1, wv_raw1, 0, GPSIMD_COLS)
+        cast_by_lines(nc.scalar.copy, wv_bf1, wv_raw1, GPSIMD_COLS, P)
         quantise(wv_bf1, P, 2 * P)
         nc.vector.tensor_copy(listed_scales[1][:], pool_scales[:].indirect(half_lists[1]))
 

@@ -27,7 +27,8 @@ GROUP = 16
 ALIGN = 64
 KIB = 1024
 GPSIMD_COLS = 32
-VECTOR_SLOTS3 = 224
+VECTOR_SLOTS3 = 192
+FIRST_SLOTS0 = 192
 
 AT_BF1 = 0
 AT_WORDS0 = AT_BF1 + KIB
@@ -200,7 +201,7 @@ def tile_attend_cachewrite_kernel(tc, emb_words, emb_scales, wv, old, retain, of
         for n, bank in enumerate(banks[2:4]):
             project(bank[:, 0:P], 0, 0, n * P, (n + 1) * P)
             nc.scalar.copy(out=values0[:, n * P : (n + 1) * P], in_=bank[:, 0:P])
-        scatter_on_scalar(window0, 0, P, values0[:, 0:P])
+        scatter_on_scalar(window0, 0, FIRST_SLOTS0, values0[:, 0:FIRST_SLOTS0])
         for half in range(2):
             project(banks[4][:, half * HALF : (half + 1) * HALF], 1, half)
         cast_by_lines(nc.vector.tensor_copy, wv_bf23, wv_raw23, 0, 2 * P)
@@ -209,7 +210,7 @@ def tile_attend_cachewrite_kernel(tc, emb_words, emb_scales, wv, old, retain, of
         scatter_on_vector(window1, 0, I, values1[:])
         project(banks[3][:, 0:HALF], 0, 1)
         nc.scalar.copy(out=values0[:, HALF:], in_=banks[3][:, 0:HALF])
-        scatter_on_scalar(window0, P, I, values0[:, P:])
+        scatter_on_scalar(window0, FIRST_SLOTS0, I, values0[:, FIRST_SLOTS0:])
 
         nc.gpsimd.tensor_tensor(kept0[:], old_sb[0][:], retain_all[:], MULT)
 
@@ -236,4 +237,4 @@ def tile_attend_cachewrite_kernel(tc, emb_words, emb_scales, wv, old, retain, of
         for b, window, pieces in ((2, window2, 2), (3, window3, 4)):
             for n in range(pieces):
                 cols = slice(n * T // pieces, (n + 1) * T // pieces)
-                add_and_store(nc.vector, nc.scalar, b, kept(b, cols), window, cols)
+                add_and_store(nc.vector, nc.sync, b, kept(b, cols), window, cols)

@@ -202,29 +202,32 @@ def tile_attend_cachewrite_kernel(tc, emb_words, emb_scales, wv, old, retain, of
             project(bank[:, 0:P], 0, 0, n * P, (n + 1) * P)
             nc.scalar.copy(out=values0[:, n * P : (n + 1) * P], in_=bank[:, 0:P])
         scatter_on_scalar(window0, 0, FIRST_SLOTS0, values0[:, 0:FIRST_SLOTS0])
-        for half in range(2):
-            project(banks[4][:, half * HALF : (half + 1) * HALF], 1, half)
+        project(banks[4][:, 0:HALF], 1, 0)
+        project(banks[3][:, 0:HALF], 0, 1)
+        project(banks[5][:, 0:HALF], 1, 1)
+        nc.scalar.copy(out=values0[:, HALF:], in_=banks[3][:, 0:HALF])
+        nc.scalar.copy(out=values1[:, HALF:], in_=banks[5][:, 0:HALF])
+        scatter_on_scalar(window0, FIRST_SLOTS0, I, values0[:, FIRST_SLOTS0:])
         cast_by_lines(nc.vector.tensor_copy, wv_bf23, wv_raw23, 0, 2 * P)
-        nc.vector.tensor_copy(values1[:], banks[4][:])
+        nc.vector.tensor_copy(values1[:, 0:HALF], banks[4][:, 0:HALF])
         quantise(wv_bf23, 2 * P, E)
         scatter_on_vector(window1, 0, I, values1[:])
-        project(banks[3][:, 0:HALF], 0, 1)
-        nc.scalar.copy(out=values0[:, HALF:], in_=banks[3][:, 0:HALF])
-        scatter_on_scalar(window0, FIRST_SLOTS0, I, values0[:, FIRST_SLOTS0:])
 
         nc.gpsimd.tensor_tensor(kept0[:], old_sb[0][:], retain_all[:], MULT)
 
         for b in (2, 3):
             for half in range(2):
                 project(banks[4 + b][:, half * HALF : (half + 1) * HALF], b, half)
-        nc.scalar.copy(out=values2[:], in_=banks[6][:])
+        nc.scalar.copy(out=values2[:, 0:HALF], in_=banks[6][:, 0:HALF])
+        nc.scalar.copy(out=values2[:, HALF:], in_=banks[6][:, HALF:])
         nc.scalar.copy(out=values3[:, 0:VECTOR_SLOTS3], in_=banks[7][:, 0:VECTOR_SLOTS3])
         scatter_on_scalar(window2, 0, HALF, values2[:, 0:HALF])
         nc.scalar.copy(out=values3[:, VECTOR_SLOTS3:], in_=banks[7][:, VECTOR_SLOTS3:])
         scatter_on_scalar(window2, HALF, I, values2[:, HALF:])
 
+        multiply_on_vector(1, 0)
         scatter_on_vector(window3, 0, VECTOR_SLOTS3, values3[:, 0:VECTOR_SLOTS3])
-        for b, h in ((1, 0), (1, 1), (2, 0)):
+        for b, h in ((1, 1), (2, 0)):
             multiply_on_vector(b, h)
         add_and_store(nc.gpsimd, nc.sync, 0, kept0[:], window0, slice(0, T))
         for h in range(2):

@@ -211,7 +211,7 @@ def tile_attend_cachewrite_kernel(tc, emb_words, emb_scales, wv, old, retain, of
         cast_by_lines(nc.vector.tensor_copy, wv_bf23, wv_raw23, 0, 2 * P)
         nc.vector.tensor_copy(values1[:, 0:HALF], banks[4][:, 0:HALF])
         quantise(wv_bf23, 2 * P, E)
-        scatter_on_vector(window1, 0, I, values1[:])
+        scatter_on_vector(window1, 0, HALF, values1[:, 0:HALF])
 
         nc.gpsimd.tensor_tensor(kept0[:], old_sb[0][:], retain_all[:], MULT)
 
@@ -226,6 +226,7 @@ def tile_attend_cachewrite_kernel(tc, emb_words, emb_scales, wv, old, retain, of
         scatter_on_scalar(window2, HALF, I, values2[:, HALF:])
 
         multiply_on_vector(1, 0)
+        scatter_on_vector(window1, HALF, I, values1[:, HALF:])
         scatter_on_vector(window3, 0, VECTOR_SLOTS3, values3[:, 0:VECTOR_SLOTS3])
         for b, h in ((1, 1), (2, 0)):
             multiply_on_vector(b, h)

@@ -27,7 +27,7 @@ GROUP = 16
 ALIGN = 64
 KIB = 1024
 GPSIMD_COLS = 32
-VECTOR_SLOTS3 = 192
+VECTOR_SLOTS3 = 224
 FIRST_SLOTS0 = 192
 
 AT_BF1 = 0

@@ -29,6 +29,9 @@ KIB = 1024
 GPSIMD_COLS = 32
 VECTOR_SLOTS3 = 224
 FIRST_SLOTS0 = 192
+CUTS1 = (0, 768, T)
+CUTS2 = (0, 256, 640, T)
+CUTS3 = (0, 256, 512, 768, T)
 
 AT_BF1 = 0
 AT_WORDS0 = AT_BF1 + KIB
@@ -38,10 +41,10 @@ QUADS_BYTES = AT_WORDS1 + ALIGN - AT_QUADS
 AT_BF0 = 48 * KIB
 AT_OLD0 = 52 * KIB
 AT_KEPT12 = 16 * KIB
-AT_BF23 = AT_KEPT12 + 6 * KIB - ALIGN
+AT_BF23 = AT_KEPT12 + 4 * KIB - ALIGN
 AT_KEPT0 = AT_BF23 + 2 * KIB - ALIGN
 AT_LATE = AT_KEPT0 + 4 * KIB - ALIGN
-AT_SCALES1 = AT_LATE + 10 * KIB
+AT_SCALES1 = AT_LATE + 12 * KIB
 AT_RAW1 = AT_BF23
 RAW1_BYTES = AT_SCALES1 + ALIGN - AT_RAW1
 
@@ -84,21 +87,17 @@ def tile_attend_cachewrite_kernel(tc, emb_words, emb_scales, wv, old, retain, of
         window2 = placed(AT_BF0, [P, T], F32, "window2")
         window3 = keep.tile([P, T], F32, name="window3")
 
-        old_sb = [placed(AT_OLD0, [P, T], F32, "old_sb0")] + [keep.tile([P, T], F32, name="old_sb%d" % b) for b in (1, 2, 3)]
+        old_sb23 = keep.tile([P, 2, T], F32, name="old_sb23")
+        old_sb = [placed(AT_OLD0, [P, T], F32, "old_sb0")] + [keep.tile([P, T], F32, name="old_sb1"), old_sb23[:, 0, :], old_sb23[:, 1, :]]
         retain_quads = placed(AT_QUADS, [P, QUADS_BYTES // 4], F32, "retain_quads")
         retain_all = keep.tile([P, T], F32, name="retain_all")
         kept0 = placed(AT_KEPT0, [P, T], F32, "kept0")
-        kept12 = placed(AT_KEPT12, [P, 3 * BANK], F32, "kept12")
-        late = placed(AT_LATE, [P, 5 * BANK], F32, "late")
-        kept_halves = [kept12[:, n * BANK : (n + 1) * BANK] for n in range(3)] + [late[:, n * BANK : (n + 1) * BANK] for n in range(3)]
-
-        def kept(b, cols):
-            h = cols.start // BANK
-            return kept_halves[2 * (b - 1) + h][:, cols.start - h * BANK : cols.stop - h * BANK]
-
+        kept1 = placed(AT_KEPT12, [P, T], F32, "kept1")
+        late = placed(AT_LATE, [P, 3 * T], F32, "late")
+        kept = [kept0[:], kept1[:], late[:, 0:T], late[:, T : 2 * T]]
         result = {b: keep.tile([P, T], F32, name="result%d" % b)[:] for b in (0, 3)}
         result[1] = placed(AT_OLD0, [P, T], F32, "result1")[:]
-        result[2] = late[:, 3 * BANK :]
+        result[2] = late[:, 2 * T :]
         ident = keep.tile([P, P], F32, name="ident")
 
         nc.vector.memset(pool_scales[:].bitcast(I32), 0)
@@ -124,8 +123,9 @@ def tile_attend_cachewrite_kernel(tc, emb_words, emb_scales, wv, old, retain, of
         load_wv(wv_raw1, P, 2 * P)
         nc.sync.dma_start(place_list[:], offs2)
         load_wv(wv_raw23[:], 2 * P, E)
-        for b in range(4):
+        for b in range(2):
             nc.sync.dma_start(out=old_sb[b][:], in_=old[b * P : (b + 1) * P, :])
+        nc.sync.dma_start(out=old_sb23[:], in_=old[2 * P :, :].rearrange("(b p) t -> p b t", p=P))
 
         def cast_by_lines(engine_copy, dst, src, lo, hi):
             engine_copy(
@@ -174,7 +174,7 @@ def tile_attend_cachewrite_kernel(tc, emb_words, emb_scales, wv, old, retain, of
 
         def multiply_on_vector(b, h):
             cols = slice(h * BANK, (h + 1) * BANK)
-            nc.vector.tensor_tensor(by_lines(kept(b, cols)), by_lines(old_sb[b][:, cols]), in_order(retain_banks[h]), MULT)
+            nc.vector.tensor_tensor(by_lines(kept[b][:, cols]), by_lines(old_sb[b][:, cols]), in_order(retain_banks[h]), MULT)
 
         def add_and_store(engine, queue, b, src, window, cols):
             engine.tensor_tensor(result[b][:, cols], src, window[:, cols], ADD)
@@ -227,18 +227,15 @@ def tile_attend_cachewrite_kernel(tc, emb_words, emb_scales, wv, old, retain, of
 
         multiply_on_vector(1, 0)
         scatter_on_vector(window1, HALF, I, values1[:, HALF:])
+        multiply_on_vector(1, 1)
         scatter_on_vector(window3, 0, VECTOR_SLOTS3, values3[:, 0:VECTOR_SLOTS3])
-        for b, h in ((1, 1), (2, 0)):
-            multiply_on_vector(b, h)
         add_and_store(nc.gpsimd, nc.sync, 0, kept0[:], window0, slice(0, T))
-        for h in range(2):
-            cols = slice(h * BANK, (h + 1) * BANK)
-            add_and_store(nc.gpsimd, nc.sync, 1, kept(1, cols), window1, cols)
+        for lo, hi in zip(CUTS1, CUTS1[1:]):
+            add_and_store(nc.gpsimd, nc.sync, 1, kept[1][:, lo:hi], window1, slice(lo, hi))
 
         scatter_on_scalar(window3, VECTOR_SLOTS3, I, values3[:, VECTOR_SLOTS3:])
-        for b, h in ((2, 1), (3, 0), (3, 1)):
+        for b, h in ((2, 0), (2, 1), (3, 0), (3, 1)):
             multiply_on_vector(b, h)
-        for b, window, pieces in ((2, window2, 2), (3, window3, 4)):
-            for n in range(pieces):
-                cols = slice(n * T // pieces, (n + 1) * T // pieces)
-                add_and_store(nc.vector, nc.sync, b, kept(b, cols), window, cols)
+        for b, window, cuts in ((2, window2, CUTS2), (3, window3, CUTS3)):
+            for lo, hi in zip(cuts, cuts[1:]):
+                add_and_store(nc.vector, nc.sync, b, kept[b][:, lo:hi], window, slice(lo, hi))

from contextlib import ExitStack

import concourse.mybir as mybir
from concourse.masks import make_identity

K, U, I, T, E = 512, 2048, 512, 1024, 512
FLOPS = 2 * K * E * I

F32 = mybir.dt.float32
BF16 = mybir.dt.bfloat16
I32 = mybir.dt.int32
U32 = mybir.dt.uint32
U16 = mybir.dt.uint16
U8 = mybir.dt.uint8
FP8X4 = mybir.dt.float8_e4m3fn_x4
FP4X4 = mybir.dt.float4_e2m1fn_x4
COPY = mybir.ActivationFunctionType.Copy
ADD = mybir.AluOpType.add
MULT = mybir.AluOpType.mult

P = 128
PACK = 4
LINE = 4
BANK = 512
HALF = I // 2
GROUP = 16
ALIGN = 64
KIB = 1024
GPSIMD_COLS = 32
VECTOR_SLOTS3 = 224
FIRST_SLOTS0 = 192
CUTS1 = (0, 768, T)
CUTS2 = (0, 256, 640, T)
CUTS3 = (0, 256, 512, 768, T)

AT_BF1 = 0
AT_WORDS0 = AT_BF1 + KIB
AT_WORDS1 = AT_WORDS0 + 2 * HALF
AT_QUADS = AT_WORDS0 - ALIGN
QUADS_BYTES = AT_WORDS1 + ALIGN - AT_QUADS
AT_BF0 = 48 * KIB
AT_OLD0 = 52 * KIB
AT_KEPT12 = 16 * KIB
AT_BF23 = AT_KEPT12 + 4 * KIB - ALIGN
AT_KEPT0 = AT_BF23 + 2 * KIB - ALIGN
AT_LATE = AT_KEPT0 + 4 * KIB - ALIGN
AT_SCALES1 = AT_LATE + 12 * KIB
AT_RAW1 = AT_BF23
RAW1_BYTES = AT_SCALES1 + ALIGN - AT_RAW1


def tile_attend_cachewrite_kernel(tc, emb_words, emb_scales, wv, old, retain, offs, offs2, out):
    nc = tc.nc
    with ExitStack() as ctx:
        keep = ctx.enter_context(tc.tile_pool(name="keep", bufs=1))
        shared = ctx.enter_context(tc.tile_pool(name="shared", bufs=1))
        psum = ctx.enter_context(tc.psum_pool(name="psum", bufs=1))

        def placed(offset, shape, dtype, name):
            return shared.tile(shape, dtype, name=name, offset=offset, align_bytes=ALIGN)

        banks = [psum.tile([P, BANK], F32, name="bank%d" % n) for n in range(8)]
        retain_banks = banks[0:2]

        emb_list = keep.tile([P, I // GROUP], U16, name="emb_list")
        place_list = keep.tile([P, I // GROUP], U16, name="place_list")
        pool_words = keep.tile([P, U], U16, name="pool_words", align_bytes=ALIGN)
        pool_scales = keep.tile([P, U], U8, name="pool_scales", align_bytes=ALIGN)
        listed_words = [placed(AT_WORDS0, [P, HALF], U16, "listed_words0"), placed(AT_WORDS1, [P, HALF], U16, "listed_words1")]
        listed_scales = [keep.tile([P, HALF], U8, name="listed_scales0", align_bytes=ALIGN), placed(AT_SCALES1, [P, HALF], U8, "listed_scales1")]

        wv_raw0 = keep.tile([P, PACK, P], F32, name="wv_raw0")
        wv_raw1 = placed(AT_RAW1, [P, RAW1_BYTES // 4], F32, "wv_raw1")[:, 0 : PACK * P].rearrange("p (j e) -> p j e", j=PACK)
        wv_raw23 = keep.tile([P, PACK, 2 * P], F32, name="wv_raw23")
        wv_bf0 = placed(AT_BF0, [P, P * PACK], BF16, "wv_bf0")
        wv_bf1 = placed(AT_BF1, [P, P * PACK], BF16, "wv_bf1")
        wv_bf23 = placed(AT_BF23, [P, 2 * P * PACK], BF16, "wv_bf23")
        wv_codes = keep.tile([P, E], U32, name="wv_codes", align_bytes=ALIGN)
        wv_scales = keep.tile([P, E], U8, name="wv_scales", align_bytes=ALIGN)

        values0 = keep.tile([P, I], F32, name="values0")
        values1 = keep.tile([P, I], F32, name="values1")
        values2 = keep.tile([P, I], F32, name="values2")
        values3 = keep.tile([P, I], F32, name="values3")
        window0 = keep.tile([P, T], F32, name="window0")
        window1 = keep.tile([P, T], F32, name="window1")
        window2 = placed(AT_BF0, [P, T], F32, "window2")
        window3 = keep.tile([P, T], F32, name="window3")

        old_sb23 = keep.tile([P, 2, T], F32, name="old_sb23")
        old_sb = [placed(AT_OLD0, [P, T], F32, "old_sb0")] + [keep.tile([P, T], F32, name="old_sb1"), old_sb23[:, 0, :], old_sb23[:, 1, :]]
        retain_quads = placed(AT_QUADS, [P, QUADS_BYTES // 4], F32, "retain_quads")
        retain_all = keep.tile([P, T], F32, name="retain_all")
        kept0 = placed(AT_KEPT0, [P, T], F32, "kept0")
        kept1 = placed(AT_KEPT12, [P, T], F32, "kept1")
        late = placed(AT_LATE, [P, 3 * T], F32, "late")
        kept = [kept0[:], kept1[:], late[:, 0:T], late[:, T : 2 * T]]
        result = {b: keep.tile([P, T], F32, name="result%d" % b)[:] for b in (0, 3)}
        result[1] = placed(AT_OLD0, [P, T], F32, "result1")[:]
        result[2] = late[:, 2 * T :]
        ident = keep.tile([P, P], F32, name="ident")

        nc.vector.memset(pool_scales[:].bitcast(I32), 0)
        nc.vector.memset(ident[:], 0.0)
        make_identity(nc, ident[:], nomemset=True)
        nc.vector.memset(window0[:], 0.0)
        nc.vector.memset(window1[:], 0.0)
        nc.vector.memset(window3[:], 0.0)

        def load_wv(dst, lo, hi):
            nc.sync.dma_start(out=dst, in_=wv[:, lo:hi].rearrange("(p j) e -> p j e", j=PACK))

        nc.sync.dma_start(
            out=retain_quads[:, 0 : 2 * LINE].rearrange("p (h c) -> p h c", c=LINE),
            in_=retain.rearrange("o (h p c) -> p (o h) c", h=2, c=LINE),
        )
        load_wv(wv_raw0[:], 0, P)
        nc.sync.dma_start(emb_list[:], offs)
        scale_rows = emb_scales[0].rearrange("(q r) u -> r q u", r=4)
        for r in range(4):
            nc.sync.dma_start(out=pool_scales[r:P:32, :].bitcast(I32), in_=scale_rows[r].bitcast(I32))
        nc.sync.dma_start(out=pool_words[:].bitcast(I32), in_=emb_words[0].bitcast(I32))
        load_wv(wv_raw1, P, 2 * P)
        nc.sync.dma_start(place_list[:], offs2)
        load_wv(wv_raw23[:], 2 * P, E)
        for b in range(2):
            nc.sync.dma_start(out=old_sb[b][:], in_=old[b * P : (b + 1) * P, :])
        nc.sync.dma_start(out=old_sb23[:], in_=old[2 * P :, :].rearrange("(b p) t -> p b t", p=P))

        def cast_by_lines(engine_copy, dst, src, lo, hi):
            engine_copy(
                out=dst[:, lo * PACK : hi * PACK].rearrange("p (c i j) -> p c j i", i=LINE, j=PACK),
                in_=src[:, :, lo:hi].rearrange("p j (c i) -> p c j i", i=LINE),
            )

        def cast_on_gpsimd(dst, src, lo, hi):
            nc.gpsimd.tensor_scalar(
                out=dst[:, lo * PACK : hi * PACK].rearrange("p (c j) -> p c j", j=PACK),
                in0=src[:, :, lo:hi].rearrange("p j c -> p c j"),
                scalar1=1.0,
                scalar2=0.0,
                op0=MULT,
                op1=ADD,
            )

        def quantise(src, lo, hi):
            nc.vector.quantize_mx(out=wv_codes[:, lo:hi].bitcast(FP8X4), scales=wv_scales[:, lo:hi], in_=src[:])

        def project(dst, b, half, lo=0, hi=HALF):
            nc.tensor.matmul_mx(
                out=dst,
                lhsT=wv_codes[:, b * P : (b + 1) * P].bitcast(FP8X4),
                lhsT_scale=wv_scales[:, b * P : (b + 1) * P],
                rhs=listed_words[half][:, lo:hi].bitcast(FP4X4),
                rhs_scale=listed_scales[half][:, lo:hi],
                start=True,
                stop=True,
            )

        def places(window, lo, hi):
            return window[:].indirect(place_list[:, lo // GROUP : hi // GROUP])

        def scatter_on_vector(window, lo, hi, src):
            nc.vector.tensor_copy(places(window, lo, hi), src)

        def scatter_on_scalar(window, lo, hi, src):
            nc.scalar.activation(places(window, lo, hi), src, COPY)

        def by_lines(cols):
            return cols.rearrange("p (n c) -> p n c", c=LINE)

        def in_order(bank):
            return bank[:].rearrange("p (c n) -> p n c", c=LINE)

        def multiply_on_vector(b, h):
            cols = slice(h * BANK, (h + 1) * BANK)
            nc.vector.tensor_tensor(by_lines(kept[b][:, cols]), by_lines(old_sb[b][:, cols]), in_order(retain_banks[h]), MULT)

        def add_and_store(engine, queue, b, src, window, cols):
            engine.tensor_tensor(result[b][:, cols], src, window[:, cols], ADD)
            queue.dma_start(out=out[b * P : (b + 1) * P, cols], in_=result[b][:, cols])

        cast_by_lines(nc.vector.tensor_copy, wv_bf0, wv_raw0, 0, P)
        for h, bank in enumerate(retain_banks):
            for c in range(LINE):
                col = h * LINE + c
                nc.tensor.transpose(bank[:, c * P : (c + 1) * P], retain_quads[:, col : col + 1].to_broadcast([P, P]), ident[:])
            nc.scalar.copy(out=by_lines(retain_all[:, h * BANK : (h + 1) * BANK]), in_=in_order(bank))

        half_lists = [emb_list[:, 0 : HALF // GROUP], emb_list[:, HALF // GROUP :]]
        nc.vector.tensor_copy(listed_scales[0][:], pool_scales[:].indirect(half_lists[0]))
        quantise(wv_bf0, 0, P)
        nc.gpsimd.memset(window2[:], 0.0)
        for half in range(2):
            nc.vector.tensor_copy(listed_words[half][:], pool_words[:].indirect(half_lists[half]))
        cast_on_gpsimd(wv_bf1, wv_raw1, 0, GPSIMD_COLS)
        cast_by_lines(nc.scalar.copy, wv_bf1, wv_raw1, GPSIMD_COLS, P)
        quantise(wv_bf1, P, 2 * P)
        nc.vector.tensor_copy(listed_scales[1][:], pool_scales[:].indirect(half_lists[1]))

        for n, bank in enumerate(banks[2:4]):
            project(bank[:, 0:P], 0, 0, n * P, (n + 1) * P)
            nc.scalar.copy(out=values0[:, n * P : (n + 1) * P], in_=bank[:, 0:P])
        scatter_on_scalar(window0, 0, FIRST_SLOTS0, values0[:, 0:FIRST_SLOTS0])
        project(banks[4][:, 0:HALF], 1, 0)
        project(banks[3][:, 0:HALF], 0, 1)
        project(banks[5][:, 0:HALF], 1, 1)
        nc.scalar.copy(out=values0[:, HALF:], in_=banks[3][:, 0:HALF])
        nc.scalar.copy(out=values1[:, HALF:], in_=banks[5][:, 0:HALF])
        scatter_on_scalar(window0, FIRST_SLOTS0, I, values0[:, FIRST_SLOTS0:])
        cast_by_lines(nc.vector.tensor_copy, wv_bf23, wv_raw23, 0, 2 * P)
        nc.vector.tensor_copy(values1[:, 0:HALF], banks[4][:, 0:HALF])
        quantise(wv_bf23, 2 * P, E)
        scatter_on_vector(window1, 0, HALF, values1[:, 0:HALF])

        nc.gpsimd.tensor_tensor(kept0[:], old_sb[0][:], retain_all[:], MULT)

        for b in (2, 3):
            for half in range(2):
                project(banks[4 + b][:, half * HALF : (half + 1) * HALF], b, half)
        nc.scalar.copy(out=values2[:, 0:HALF], in_=banks[6][:, 0:HALF])
        nc.scalar.copy(out=values2[:, HALF:], in_=banks[6][:, HALF:])
        nc.scalar.copy(out=values3[:, 0:VECTOR_SLOTS3], in_=banks[7][:, 0:VECTOR_SLOTS3])
        scatter_on_scalar(window2, 0, HALF, values2[:, 0:HALF])
        nc.scalar.copy(out=values3[:, VECTOR_SLOTS3:], in_=banks[7][:, VECTOR_SLOTS3:])
        scatter_on_scalar(window2, HALF, I, values2[:, HALF:])

        multiply_on_vector(1, 0)
        scatter_on_vector(window1, HALF, I, values1[:, HALF:])
        multiply_on_vector(1, 1)
        scatter_on_vector(window3, 0, VECTOR_SLOTS3, values3[:, 0:VECTOR_SLOTS3])
        add_and_store(nc.gpsimd, nc.sync, 0, kept0[:], window0, slice(0, T))
        for lo, hi in zip(CUTS1, CUTS1[1:]):
            add_and_store(nc.gpsimd, nc.sync, 1, kept[1][:, lo:hi], window1, slice(lo, hi))

        scatter_on_scalar(window3, VECTOR_SLOTS3, I, values3[:, VECTOR_SLOTS3:])
        for b, h in ((2, 0), (2, 1), (3, 0), (3, 1)):
            multiply_on_vector(b, h)
        for b, window, cuts in ((2, window2, CUTS2), (3, window3, CUTS3)):
            for lo, hi in zip(cuts, cuts[1:]):
                add_and_store(nc.vector, nc.sync, b, kept[b][:, lo:hi], window, slice(lo, hi))
